import numpy as np, ml_dtypes
CORES = [10,34,74,98]
N = 4
BF = ml_dtypes.bfloat16
def gentries(a):
    return np.ascontiguousarray(a.reshape(8, 16, -1).transpose(0, 2, 1)).reshape(8, -1)
def gtable(e):
    e = np.asarray(e); return np.ascontiguousarray(e.reshape(8, -1, 16).transpose(0, 2, 1)).reshape(128, -1).astype(np.int32)
K, D, SH = 1024, 4096, 4
def sized(rng):
    return rng.standard_normal((N, 128, D), dtype=np.float32) * np.exp2(rng.integers(-1, 2, (N, 128, 1))).astype(np.float32)
def hashes(a, b):
    return np.repeat(np.stack([a, b], 2), 16, axis=1).astype(np.int32)
def lists(e):
    return np.stack([gtable(u) for u in e])
def setup_inputs(rng):
    a = np.stack([rng.permutation(255)[:8] + 1 for r in range(N)]); b = rng.integers(0, 65536, (N, 8))
    return {"mat": sized(rng).astype(BF), "ids": lists(rng.integers(0, 65536, (N, 8, K))), "hs": hashes(a, b)}
def setup_inputs_ends(rng):
    e = rng.integers(0, 65536, (N, 8, K)); e = np.where(rng.random(e.shape) < 0.5, rng.choice(np.array([0, 1, 65534, 65535]), e.shape), e)
    e[:, :, 0] = 0; e[:, :, 1] = 1 << SH; e[:, :, -1] = 65535
    top = (D - 1) << SH; low = (1 << SH) - 1
    a = rng.choice(np.array([0, 1, 254, 255]), (N, 8)); b = rng.choice(np.array([0, 1, low, top, top + low, 65535]), (N, 8))
    for r in range(N):
        a[r, r % 8], b[r, r % 8] = 1, top
        a[r, (r + 1) % 8], b[r, (r + 1) % 8] = 255, 65535
        a[r, (r + 2) % 8] = 0
        a[r, (r + 3) % 8], b[r, (r + 3) % 8] = 1, top + low
    return {"mat": sized(rng).astype(BF), "ids": lists(e), "hs": hashes(a, b)}
def setup_inputs_one(rng):
    d = setup_inputs(rng); e = rng.integers(0, 65536, (N, 8, K)); o = rng.permutation(N)
    e[o[0]] = rng.permutation(65536)[:8, None]; e[o[1]] = e[o[2]]; e[o[3]] = np.repeat(e[o[3], :, :K // 16], 16, axis=1)
    d["ids"] = lists(e); d["hs"][rng.integers(0, N), :, 0] = 0; return d
def setup_inputs_turns(rng):
    d = setup_inputs(rng); p = np.argsort(rng.random((N, 8, D, 4)), axis=3)
    w = (rng.integers(128, 256, p.shape) * (2 * rng.integers(0, 2, p.shape) - 1)).astype(np.float32) * np.float32(2.0 ** -7)
    m = np.where(p[..., None] == np.arange(4), w[..., None], np.float32(0))
    d["mat"] = np.ascontiguousarray(m.transpose(0, 1, 3, 4, 2)).reshape(N, 128, D).astype(BF); return d
def setup_inputs_spread(rng):
    d = setup_inputs(rng); k = (N, 8, 1, D)
    z = (np.exp2(rng.integers(-2, 3, k)) * (rng.random(k) > 0.03125)).astype(np.float32)
    d["mat"] = (sized(rng).reshape(N, 8, 16, D) * z).reshape(N, 128, D).astype(BF); return d
def check_inputs(d):
    bad = []; h = d["hs"].reshape(N, 8, 16, 2)
    if not (np.abs(d["mat"].astype(np.float32)) <= 8192).all(): bad.append("size of mat")
    if not ((d["ids"] >= 0) & (d["ids"] <= 65535)).all(): bad.append("range of ids")
    if not ((h >= 0) & (h <= np.array([255, 65535]))).all(): bad.append("range of hs")
    if not (h == h[:, :, :1]).all(): bad.append("rows of hs alike in a group")
    return bad
def reference(mat, ids, hs):
    y = np.zeros((N, 32, K), np.float64); m = mat.astype(np.float64).reshape(N, 8, 16, D); h = hs.astype(np.int64)[:, ::16]
    for r in range(N):
        i = gentries(ids[r]).astype(np.int64)
        v = np.zeros((8, 4, K), np.float64); v[:, 0] = 1
        for q in range(N):
            t = ((i * h[q, :, :1] + h[q, :, 1:]) >> SH) & (D - 1)
            x = np.take_along_axis(m[q], t[:, None, :], 2).reshape(8, 4, 4, K)
            v = np.sum(v[:, :, None, :] * x, axis=1)
        y[r] = v.reshape(32, K)
    return {"y": y.astype(np.float32)}

@@ -1,0 +1,315 @@
+from concourse.mybir import AluOpType, ActivationFunctionType
+
+N = 4
+K = 1024
+C = 256
+NC = K // C
+L = K // 16
+A = AluOpType
+
+SCRATCH = {
+    "idl": ("sbuf", [128, N * L], "int32"),
+    "hsi": ("sbuf", [128, 2], "int32"),
+    "hsf": ("sbuf", [128, 2], "float32"),
+    "win": ("sbuf", [128, 4096], "bfloat16"),
+    "t1": ("sbuf", [128, N * L], "int32"),
+    "t2": ("sbuf", [128, N * L], "int32"),
+    "offs": ("sbuf", [128, N * L], "uint16"),
+    "gat": ("sbuf", [128, N * K], "bfloat16"),
+    "land": ("sbuf", [128, N * K], "bfloat16"),
+    "c0s": ("sbuf", [128, N * 256], "bfloat16"),
+    "c0l": ("sbuf", [128, 256], "bfloat16"),
+    "hi": ("sbuf", [128, K], "bfloat16"),
+    "lo": ("sbuf", [128, K], "bfloat16"),
+    "p1": ("sbuf", [128, K], "float32"),
+    "p2": ("sbuf", [128, K], "float32"),
+    "p3": ("sbuf", [128, K], "float32"),
+    "yb": ("sbuf", [128, NC * 64], "float32"),
+    "km": ("sbuf", [128, 128], "float32"),
+    "m32": ("sbuf", [128, 32], "float32"),
+    "pidx": ("sbuf", [128, 1], "int32"),
+    "i1": ("sbuf", [128, 1], "int32"),
+    "i2": ("sbuf", [128, 1], "int32"),
+    "i3": ("sbuf", [128, 1], "int32"),
+    "keyp": ("sbuf", [128, 1], "float32"),
+    "key0": ("sbuf", [128, 1], "float32"),
+    "sf": ("sbuf", [128, 128], "float32"),
+    "sb": ("sbuf", [128, 128], "bfloat16"),
+    "so": ("sbuf", [128, 32], "float32"),
+    "ex": ("sbuf", [128, 512], "bfloat16"),
+    "cm": ("sbuf", [128, 512], "bfloat16"),
+}
+for _b in range(NC):
+    SCRATCH["pa%d" % _b] = ("psum", [128, 2 * C], "float32")
+    SCRATCH["pb%d" % _b] = ("psum", [128, 2 * C], "float32")
+SEMAPHORES = (["e%d" % i for i in range(118)] + ["ida%d" % r for r in range(N)]
+              + ["ma%d_%d" % (q, b) for q in range(1, N) for b in range(NC)]
+              + ["rl%d" % i for i in range(10)] + ["va", "ls", "st"])
+
+IDS_TO = {0: [2, 1, 3], 1: [0, 3, 2], 2: [1, 0, 3], 3: [0, 1, 2]}
+SERVE = {0: [1, 3, 2], 1: [2, 3, 0], 2: [0, 1, 3], 3: [2, 1, 0]}
+PLAN = {1: [(2, 0, 3, -1), (2, 3, 4, 0), (3, 0, 3, -1), (3, 3, 4, 1), (0, 0, 3, -1), (0, 3, 4, 0)],
+        2: [(0, 0, 2, -1), (0, 2, 3, -1), (1, 3, 4, 1), (0, 3, 4, 0), (1, 0, 3, -1), (3, 0, 3, -1), (3, 3, 4, 0)],
+        3: [(2, 0, 3, -1), (2, 3, 4, 0), (1, 0, 3, -1), (1, 3, 4, 1), (0, 0, 2, -1), (0, 2, 3, 0), (0, 3, 4, 0)]}
+HALF = (("v", 0, 2), ("s", 2, 4))
+SPLIT = {0: (("v", 0, 1), ("s", 1, 3), ("s", 3, 4)), 1: (("v", 0, 1), ("s", 1, 2), ("v", 2, 3), ("s", 3, 4)),
+         2: (("v", 0, 1), ("v", 1, 2), ("s", 2, 3), ("s", 3, 4)), 3: (("v", 3, 4), ("s", 0, 1), ("s", 1, 3))}
+WHOLE = {0: (0,), 1: (0, 1), 2: (0,), 3: (0, 2)}
+ORDER = {0: "m10 m11 lo1 m20 m21 m12 m13 lo2 m30 lo3 m31 m22 ou0 m23 ou1 m32 m33 ou2 ou3",
+         1: "m10 m11 m12 m13 lo2 lo3 m21 m22 m20 m23 m30 m31 ou0 m32 ou1 m33 ou2 ou3",
+         2: "m10 m11 m12 lo1 m20 m13 lo2 m21 lo3 m22 m30 m23 m31 ou0 m32 m33 ou1 ou2 ou3",
+         3: "m10 m11 m12 m20 lo1 m13 m30 m21 lo3 m22 m31 ou0 m23 ou1 m32 m33 ou2 ou3"}
+
+
+def relays_of(core, T, topo):
+    c = [x for x in topo.cores_of(core) if x != core and all(topo.may_write(x, d) for d in T.cores)]
+    return [x for x in c if topo.die(x) != topo.die(core)] + [x for x in c if topo.die(x) == topo.die(core)]
+
+
+def inner_engines(core, relay, dst, topo):
+    return [e for e in topo.engines(core, relay) if e not in topo.engines(core, dst)]
+
+
+def relay_program(g, core, q, way, T, topo):
+    sent = 0
+    for i, (r, c0, c1, w) in enumerate(PLAN[q]):
+        if w != way:
+            continue
+        dst = T.cores[r]
+        rid, pid, _se = topo.addr(dst)
+        g.wait_ge(T.sem["rl%d" % i], len(inner_engines(T.cores[q], core, dst, topo)))
+        g.remote_dma(T.land[:, q * K + c0 * C:q * K + c1 * C], T.gat[:, r * K + c0 * C:r * K + c1 * C],
+                     T.sem["ma%d_%d" % (q, c0)], T.sem["ls"], pid, rid, topo.mask(core, dst))
+        sent += len(topo.engines(core, dst))
+    if sent:
+        g.wait_ge(T.sem["ls"], sent)
+
+
+def rank_program(g, core, T, topo):
+    rank = T.rank_of(core)
+    if rank is None:
+        for q in PLAN:
+            relays = relays_of(T.cores[q], T, topo)
+            if core in relays:
+                relay_program(g, core, q, relays.index(core), T, topo)
+        return
+    vec, act, ten, sync = g.vector, g.scalar, g.tensor, g.sync
+    used = [0]
+
+    def ev(ins, n=1):
+        name = "e%d" % used[0]
+        used[0] += 1
+        ins.then_inc(T.sem[name], n)
+        return (name, n)
+
+    def wait(q, *evs):
+        for name, n in evs:
+            q.wait_ge(T.sem[name], n)
+
+    sent = [0]
+
+    def send(dst_rank, out_ap, in_ap, sem):
+        dst = T.cores[dst_rank]
+        rid, pid, _se = topo.addr(dst)
+        g.remote_dma(out_ap, in_ap, T.sem[sem], T.sem["ls"], pid, rid, topo.mask(core, dst))
+        sent[0] += len(topo.engines(core, dst))
+
+    def arrived(src_rank, sem):
+        return (sem, len(topo.engines(T.cores[src_rank], core)))
+
+    def slot(buf, r, w):
+        return buf[:, r * w:(r + 1) * w]
+
+    e_ids = ev(sync.dma_start(slot(T.idl, rank, L), T.ids[:]), 16)
+    e_hs = ev(act.dma_start(T.hsi[:], T.hs[:]), 16)
+    e_mat = ev(sync.dma_start(T.win[:], T.mat[:]), 16)
+
+    e_p = ev(g.iota(T.pidx[:], [[1, 1]], 0, 1))
+    e_km = ev(g.iota(T.km[:], [[1, 32], [0, 4]], 0, 0, allow_small_or_imprecise_dtypes=True))
+    e_m32 = ev(g.iota(T.m32[:], [[1, 32]], 0, 0, allow_small_or_imprecise_dtypes=True))
+    wait(g, e_ids)
+    for r in IDS_TO[rank]:
+        send(r, slot(T.idl, rank, L), slot(T.idl, rank, L), "ida%d" % rank)
+
+    wait(vec, e_p)
+    e1 = ev(vec.tensor_scalar(T.i1[:], T.pidx[:], 2, 28, A.logical_shift_right, A.bitwise_and))
+    e2 = ev(vec.tensor_scalar(T.i2[:], T.pidx[:], 3, None, A.bitwise_and))
+    wait(vec, e1, e2)
+    e_key = ev(vec.tensor_tensor(T.keyp[:], T.i1[:], T.i2[:], A.add))
+    if rank == 0:
+        e3 = ev(vec.tensor_scalar(T.i3[:], T.pidx[:], 12, None, A.bitwise_and))
+        wait(vec, e3, e_key)
+        e_k0 = ev(vec.tensor_scalar(T.key0[:], T.i3[:], 100.0, T.keyp[:, 0:1], A.mult, A.add))
+    else:
+        e_k0 = ev(vec.tensor_copy(T.key0[:], T.pidx[:]))
+        wait(vec, e_key)
+    wait(vec, e_km, e_m32)
+    e_sb = ev(vec.tensor_scalar(T.sb[:], T.km[:], T.keyp[:, 0:1], None, A.is_equal))
+    e_sf = ev(vec.tensor_scalar(T.sf[:], T.km[:], T.keyp[:, 0:1], None, A.is_equal))
+    e_so = ev(vec.tensor_scalar(T.so[:], T.m32[:], T.keyp[:, 0:1], None, A.is_equal))
+    wait(vec, e_k0)
+    consts = [e_sb, e_sf, e_so]
+    if rank == 0:
+        consts.append(ev(vec.tensor_scalar(T.ex[:, 0:128], T.km[:], T.key0[:, 0:1], None, A.is_equal)))
+        e_c = ev(vec.memset(T.cm[:], 0.0))
+        wait(vec, e_c)
+        for b in range(4):
+            o = 128 * b + 32 * b
+            consts.append(ev(vec.tensor_scalar(T.cm[:, o:o + 32], T.m32[:], T.key0[:, 0:1], None, A.is_equal)))
+    else:
+        for b in range(4):
+            consts.append(ev(vec.tensor_scalar(T.ex[:, 128 * b:128 * b + 128], T.km[:], float(32 * b), T.key0[:, 0:1],
+                                               A.add, A.is_equal)))
+    wait(ten, *consts)
+
+    wait(vec, e_hs)
+    e_hf = ev(vec.tensor_copy(T.hsf[:], T.hsi[:]))
+    wait(vec, e_hf)
+
+    gathered = {}
+
+    def hash_list(r):
+        wait(vec, e_ids if r == rank else arrived(r, "ida%d" % r))
+        a = ev(vec.tensor_scalar(slot(T.t1, r, L), slot(T.idl, r, L), T.hsf[:, 0:1], T.hsf[:, 1:2], A.mult, A.add))
+        wait(vec, a)
+        b = ev(vec.tensor_scalar(slot(T.t2, r, L), slot(T.t1, r, L), 4, 4095, A.logical_shift_right, A.bitwise_and))
+        wait(vec, b)
+        c = ev(vec.tensor_copy(slot(T.offs, r, L), slot(T.t2, r, L)))
+        wait(vec, c)
+        wait(act, c)
+        if r == rank:
+            wait(vec, e_mat)
+            wait(act, e_mat)
+
+    def gather(r, split):
+        gathered[r] = {}
+        for q, b0, b1 in split:
+            dst = T.gat[:, r * K + b0 * C:r * K + b1 * C]
+            src = T.win[:].indirect(T.offs[:, r * L + b0 * C // 16:r * L + b1 * C // 16])
+            e = ev(vec.tensor_copy(dst, src) if q == "v" else act.activation(dst, src, ActivationFunctionType.Copy))
+            for b in range(b0, b1):
+                gathered[r][b] = e
+
+    hash_list(rank)
+    gather(rank, HALF)
+    PA = [T["pa%d" % b] for b in range(NC)]
+    PB = [T["pb%d" % b] for b in range(NC)]
+    left, right = slice(0, C), slice(C, 2 * C)
+    col = [slice(b * C, (b + 1) * C) for b in range(NC)]
+    e_v0 = {}
+    if rank == 0:
+        for b in range(NC):
+            wait(ten, gathered[0][b])
+            e_v0[b] = ev(ten.matmul(PA[b][:, left], T.ex[:, 0:128], T.gat[:, col[b]], True, True))
+        copies, packed = [], []
+
+        def unload(i):
+            r = SERVE[0][i]
+            wait(vec, packed[i])
+            e = ev(vec.tensor_copy(slot(T.c0s, r, 256), PB[i][:, 0:256]))
+            copies.append(e)
+            wait(g, e)
+            send(r, T.c0l[:], slot(T.c0s, r, 256), "va")
+
+        for i, r in enumerate(SERVE[0]):
+            hash_list(r)
+            gather(r, SPLIT[0])
+            ins = None
+            for b in range(NC):
+                wait(ten, gathered[r][b])
+                m = r * K + b * C
+                ins = ten.matmul(PB[i][:, 0:256], T.cm[:, 128 * b:128 * b + 128], T.gat[:, m:m + C], b == 0, b == NC - 1)
+            packed.append(ev(ins))
+            if i:
+                unload(i - 1)
+        unload(N - 2)
+        wait(ten, *copies)
+    else:
+        for r in SERVE[rank]:
+            hash_list(r)
+            gather(r, SPLIT[rank])
+        relays = relays_of(core, T, topo)
+        for i, (r, c0, c1, way) in enumerate(PLAN[rank]):
+            wait(g, *sorted(set(gathered[r][b] for b in range(c0, c1))))
+            m = slice(r * K + c0 * C, r * K + c1 * C)
+            if way < 0:
+                send(r, T.land[:, rank * K + c0 * C:rank * K + c1 * C], T.gat[:, m], "ma%d_%d" % (rank, c0))
+            else:
+                rid, pid, _se = topo.addr(relays[way])
+                eng = inner_engines(core, relays[way], T.cores[r], topo)
+                g.remote_dma(T.gat[:, m], T.gat[:, m], T.sem["rl%d" % i], T.sem["ls"], pid, rid, sum(1 << e for e in eng))
+                sent[0] += len(eng)
+        wait(ten, arrived(0, "va"))
+        for b in range(NC):
+            e_v0[b] = ev(ten.matmul(PA[b][:, left], T.ex[:, 128 * b:128 * b + 128], T.c0l[:], True, True))
+
+    came = {}
+    for q in PLAN:
+        for r, c0, c1, way in PLAN[q]:
+            if r == rank:
+                src = T.cores[q] if way < 0 else relays_of(T.cores[q], T, topo)[way]
+                for b in range(c0, c1):
+                    came[q, b] = ("ma%d_%d" % (q, c0), len(topo.engines(src, core)))
+
+    def picks(s, b):
+        m = s * K + b * C
+        if s == rank:
+            return T.gat[:, m:m + C], gathered[rank][b]
+        return T.land[:, m:m + C], came[s, b]
+
+    e_hi, e_mm, e_fin = {}, {}, {}
+
+    def m1(b):
+        ap, e = picks(1, b)
+        wait(vec, e_v0[b], e)
+        if b in WHOLE[rank]:
+            e = ev(vec.tensor_tensor(T.p1[:, col[b]], PA[b][:, left], ap, A.mult))
+            wait(ten, e)
+            e_mm[1, b] = ev(ten.matmul(PB[b][:, left], T.sf[:], T.p1[:, col[b]], True, True))
+        else:
+            e = ev(vec.tensor_tensor(PA[b][:, right], PA[b][:, left], ap, A.mult))
+            wait(act, e)
+            e_hi[b] = ev(act.activation(T.hi[:, col[b]], PA[b][:, right], ActivationFunctionType.Copy))
+
+    def lo(b):
+        wait(vec, e_hi[b])
+        e = ev(vec.tensor_tensor(T.lo[:, col[b]], PA[b][:, right], T.hi[:, col[b]], A.subtract))
+        wait(ten, e_hi[b])
+        ten.matmul(PB[b][:, left], T.sb[:], T.hi[:, col[b]], True, False)
+        wait(ten, e)
+        e_mm[1, b] = ev(ten.matmul(PB[b][:, left], T.sb[:], T.lo[:, col[b]], False, True))
+
+    def m2(b):
+        ap, e = picks(2, b)
+        wait(vec, e_mm[1, b], e)
+        e = ev(vec.tensor_tensor(T.p2[:, col[b]], PB[b][:, left], ap, A.mult))
+        wait(ten, e)
+        e_mm[2, b] = ev(ten.matmul(PB[b][:, right], T.sf[:], T.p2[:, col[b]], True, True))
+
+    def m3(b):
+        ap, e = picks(3, b)
+        wait(vec, e_mm[2, b], e)
+        e = ev(vec.tensor_tensor(T.p3[:, col[b]], PB[b][:, right], ap, A.mult))
+        wait(ten, e)
+        e_fin[b] = [ev(ten.matmul(PA[b][:, 32 * j:32 * j + 32], T.p3[:, b * C + j:(b + 1) * C:2], T.so[:], True, True))
+                    for j in range(2)]
+
+    stored = []
+
+    def out(b):
+        wait(vec, *e_fin[b])
+        for j in range(2):
+            e = ev(vec.transpose(T.yb[:, 64 * b + j:64 * b + 64:2], PA[b][:, 32 * j:32 * j + 32]))
+            wait(sync, e)
+            wait(act, e)
+        for a in range(4):
+            q = act if a % 2 else sync
+            o = b * C + 64 * a
+            q.dma_start(T.y[:, o:o + 64], T.yb[32 * a:32 * a + 32, 64 * b:64 * b + 64]).then_inc(T.sem["st"], 16)
+            stored.append(16)
+
+    do = {"m1": m1, "lo": lo, "m2": m2, "m3": m3, "ou": out}
+    for step in ORDER[rank].split():
+        do[step[:2]](int(step[2]))
+    wait(sync, ("st", sum(stored)))
+    wait(g, ("ls", sent[0]))

@@ -9,7 +9,9 @@ A = AluOpType
 
 SCRATCH = {
     "idl": ("sbuf", [128, N * L], "int32"),
-    "hsi": ("sbuf", [128, 2], "int32"),
+    "hri": ("sbuf", [128, 256], "int32"),
+    "hrf": ("sbuf", [128, 256], "float32"),
+    "one": ("sbuf", [128, 1], "float32"),
     "hsf": ("sbuf", [128, 2], "float32"),
     "win": ("sbuf", [128, 4096], "bfloat16"),
     "t1": ("sbuf", [128, N * L], "int32"),
@@ -42,43 +44,71 @@ SCRATCH = {
 for _b in range(NC):
     SCRATCH["pa%d" % _b] = ("psum", [128, 2 * C], "float32")
     SCRATCH["pb%d" % _b] = ("psum", [128, 2 * C], "float32")
-SEMAPHORES = (["e%d" % i for i in range(118)] + ["ida%d" % r for r in range(N)]
-              + ["ma%d_%d" % (q, b) for q in range(1, N) for b in range(NC)]
-              + ["rl%d" % i for i in range(10)] + ["va", "ls", "st"])
+SEMAPHORES = (["e%d" % i for i in range(126)] + ["ida%d" % r for r in range(N)]
+              + ["ma%d_%d" % (q, b) for q in range(N) for b in range(NC)] + ["ls", "st", "co"])
 
-IDS_TO = {0: [2, 1, 3], 1: [0, 3, 2], 2: [1, 0, 3], 3: [0, 1, 2]}
-SERVE = {0: [1, 3, 2], 1: [2, 3, 0], 2: [0, 1, 3], 3: [2, 1, 0]}
-PLAN = {1: [(2, 0, 3, -1), (2, 3, 4, 0), (3, 0, 3, -1), (3, 3, 4, 1), (0, 0, 3, -1), (0, 3, 4, 0)],
-        2: [(0, 0, 2, -1), (0, 2, 3, -1), (1, 3, 4, 1), (0, 3, 4, 0), (1, 0, 3, -1), (3, 0, 3, -1), (3, 3, 4, 0)],
-        3: [(2, 0, 3, -1), (2, 3, 4, 0), (1, 0, 3, -1), (1, 3, 4, 1), (0, 0, 2, -1), (0, 2, 3, 0), (0, 3, 4, 0)]}
-HALF = (("v", 0, 2), ("s", 2, 4))
-SPLIT = {0: (("v", 0, 1), ("s", 1, 3), ("s", 3, 4)), 1: (("v", 0, 1), ("s", 1, 2), ("v", 2, 3), ("s", 3, 4)),
-         2: (("v", 0, 1), ("v", 1, 2), ("s", 2, 3), ("s", 3, 4)), 3: (("v", 3, 4), ("s", 0, 1), ("s", 1, 3))}
-WHOLE = {0: (0,), 1: (0, 1), 2: (0,), 3: (0, 2)}
-ORDER = {0: "m10 m11 lo1 m20 m21 m12 m13 lo2 m30 lo3 m31 m22 ou0 m23 ou1 m32 m33 ou2 ou3",
-         1: "m10 m11 m12 m13 lo2 lo3 m21 m22 m20 m23 m30 m31 ou0 m32 ou1 m33 ou2 ou3",
-         2: "m10 m11 m12 lo1 m20 m13 lo2 m21 lo3 m22 m30 m23 m31 ou0 m32 m33 ou1 ou2 ou3",
-         3: "m10 m11 m12 m20 lo1 m13 m30 m21 lo3 m22 m31 ou0 m23 ou1 m32 m33 ou2 ou3"}
-
-
-def relays_of(core, T, topo):
-    c = [x for x in topo.cores_of(core) if x != core and all(topo.may_write(x, d) for d in T.cores)]
-    return [x for x in c if topo.die(x) != topo.die(core)] + [x for x in c if topo.die(x) == topo.die(core)]
+IDS_TO = {0: "132", 1: "023", 2: "301", 3: "210"}
+PLAN = {0: "102d 202d 302d 224d 324d 124d",
+        1: "002d 024a 302d 202d 324b 224d",
+        2: "302d 324a 002d 102d 024b 124d",
+        3: "202d 224a 102d 002d 124b 024d"}
+WHOLE = {0: "23", 1: "0123", 2: "123", 3: "0123"}
+PROG = {0: "h0 v002 e0 s024 e2 e1 e3 h1 s102 h2 p102 h3 v302 s202 p202 u102 p302 s124 U202 U302 v223 v234 p124 s324 "
+           "U124 p224 u224 p324 u324 "
+           "m10 m11 lo0 lo1 A20 A21 B20 B21 A30 B30 A12 B31 B12 A31 m13 A22 B22 m23 A32 ou1 ou0 B32 A33 B33 ou2 ou3",
+        1: "h1 v102 s124 h0 s002 s023 v034 h32 v302 s202 e0 s324 s234 e1 m11 m10 s223 "
+           "m21 A20 B20 A31 B31 A30 B30 ou1 ou0 e2 e3 A12 A13 B12 A22 B13 B22 B23 A23 A32 B33 B32 A33 ou2 ou3",
+        2: "h2 h3 v202 s224 s302 x1 x0 y0 y1 z0 s324 z1 v002 s102 e1 s123 s024 e0 s134 "
+           "A11 B11 m10 A21 B21 lo0 A31 B31 ou1 e2 e3 A12 B12 m13 m20 A22 B22 A23 B23 A30 B30 A32 B32 A33 B33 ou0 ou2 ou3",
+        3: "h3 v302 s324 h2 s202 v234 h10 v223 s034 s003 v102 e0 v124 e1 "
+           "A10 A11 B10 B11 A20 B20 A21 B21 A30 B30 A31 ou0 e2 e3 B31 A12 B12 m13 ou1 A22 B22 A23 B23 A32 B32 A33 B33 "
+           "ou2 ou3"}
+NEAR, FAR = "abcefg", "mnop"
 
 
-def inner_engines(core, relay, dst, topo):
-    return [e for e in topo.engines(core, relay) if e not in topo.engines(core, dst)]
+def plan(q):
+    return [(int(w[0]), int(w[1]), int(w[2]), w[3]) for w in PLAN[q].split()]
 
 
-def relay_program(g, core, q, way, T, topo):
+def hash_slot(q, r):
+    return "".join(w[1:] for w in PROG[q].split() if w[0] in "hx").index(str(r))
+
+
+def relay(q, r, way, T, topo):
+    src, dst = T.cores[q], T.cores[r]
+    if way == "d":
+        return src
+    if way in NEAR:
+        c = [x for x in topo.cores_of(src) if x != src]
+        c.sort(key=lambda x: (not all(topo.may_write(x, d) for d in T.cores), topo.die(x) == topo.die(src)))
+        return c[NEAR.index(way)]
+    c = [x for x in range(topo.CHIPS * topo.CORES_PER_CHIP)
+         if topo.mates(topo.chip(x), topo.chip(dst)) and topo.may_write(x, dst)]
+    c.sort(key=lambda x: topo.die(x) == topo.die(dst))
+    return c[FAR.index(way)]
+
+
+def first_engines(q, r, way, T, topo):
+    src, via = T.cores[q], relay(q, r, way, T, topo)
+    eng = topo.engines(src, via)
+    return [e for e in eng if e not in topo.engines(src, T.cores[r])] if way in NEAR else eng
+
+
+def held(T, q, r, c0, c1, way):
+    buf, s = (T.gat, r) if way in NEAR else (T.land, q)
+    return buf[:, s * K + c0 * C:s * K + c1 * C]
+
+
+def relay_program(g, core, T, topo):
     sent = 0
-    for i, (r, c0, c1, w) in enumerate(PLAN[q]):
-        if w != way:
+    for i, q in sorted((i, q) for q in range(1, N) for i in range(len(plan(q)))):
+        r, c0, c1, way = plan(q)[i]
+        if relay(q, r, way, T, topo) != core:
             continue
         dst = T.cores[r]
         rid, pid, _se = topo.addr(dst)
-        g.wait_ge(T.sem["rl%d" % i], len(inner_engines(T.cores[q], core, dst, topo)))
-        g.remote_dma(T.land[:, q * K + c0 * C:q * K + c1 * C], T.gat[:, r * K + c0 * C:r * K + c1 * C],
+        g.wait_ge(T.sem["e%d" % (16 * q + i)], len(first_engines(q, r, way, T, topo)))
+        g.remote_dma(T.land[:, q * K + c0 * C:q * K + c1 * C], held(T, q, r, c0, c1, way),
                      T.sem["ma%d_%d" % (q, c0)], T.sem["ls"], pid, rid, topo.mask(core, dst))
         sent += len(topo.engines(core, dst))
     if sent:
@@ -88,13 +118,11 @@ def relay_program(g, core, q, way, T, topo):
 def rank_program(g, core, T, topo):
     rank = T.rank_of(core)
     if rank is None:
-        for q in PLAN:
-            relays = relays_of(T.cores[q], T, topo)
-            if core in relays:
-                relay_program(g, core, q, relays.index(core), T, topo)
+        relay_program(g, core, T, topo)
         return
     vec, act, ten, sync = g.vector, g.scalar, g.tensor, g.sync
     used = [0]
+    seen = set()
 
     def ev(ins, n=1):
         name = "e%d" % used[0]
@@ -102,214 +130,284 @@ def rank_program(g, core, T, topo):
         ins.then_inc(T.sem[name], n)
         return (name, n)
 
+    names = {"v": vec, "s": act, "t": ten, "y": sync, "g": g}
+
     def wait(q, *evs):
         for name, n in evs:
-            q.wait_ge(T.sem[name], n)
+            if (q, name) not in seen:
+                seen.add((q, name))
+                names[q].wait_ge(T.sem[name], n)
 
     sent = [0]
 
-    def send(dst_rank, out_ap, in_ap, sem):
-        dst = T.cores[dst_rank]
+    def send(dst, out_ap, in_ap, sem, eng):
         rid, pid, _se = topo.addr(dst)
-        g.remote_dma(out_ap, in_ap, T.sem[sem], T.sem["ls"], pid, rid, topo.mask(core, dst))
-        sent[0] += len(topo.engines(core, dst))
+        g.remote_dma(out_ap, in_ap, T.sem[sem], T.sem["ls"], pid, rid, sum(1 << e for e in eng))
+        sent[0] += len(eng)
 
-    def arrived(src_rank, sem):
-        return (sem, len(topo.engines(T.cores[src_rank], core)))
+    def slot(buf, r, w, n=1):
+        return buf[:, r * w:(r + n) * w]
 
-    def slot(buf, r, w):
-        return buf[:, r * w:(r + 1) * w]
-
-    e_ids = ev(sync.dma_start(slot(T.idl, rank, L), T.ids[:]), 16)
-    e_hs = ev(act.dma_start(T.hsi[:], T.hs[:]), 16)
+    own = slot(T.idl, hash_slot(rank, rank), L)
+    e_ids = ev(sync.dma_start(own, T.ids[:]), 16)
+    e_hs = ev(act.dma_start(T.hri[0:1, :], T.hs[:]), 16)
     e_mat = ev(sync.dma_start(T.win[:], T.mat[:]), 16)
 
     e_p = ev(g.iota(T.pidx[:], [[1, 1]], 0, 1))
     e_km = ev(g.iota(T.km[:], [[1, 32], [0, 4]], 0, 0, allow_small_or_imprecise_dtypes=True))
     e_m32 = ev(g.iota(T.m32[:], [[1, 32]], 0, 0, allow_small_or_imprecise_dtypes=True))
-    wait(g, e_ids)
-    for r in IDS_TO[rank]:
-        send(r, slot(T.idl, rank, L), slot(T.idl, rank, L), "ida%d" % rank)
+    wait("g", e_ids)
+    for r in map(int, IDS_TO[rank]):
+        send(T.cores[r], slot(T.idl, hash_slot(r, rank), L), own, "ida%d" % rank, topo.engines(core, T.cores[r]))
 
-    wait(vec, e_p)
+    wait("v", e_p)
     e1 = ev(vec.tensor_scalar(T.i1[:], T.pidx[:], 2, 28, A.logical_shift_right, A.bitwise_and))
     e2 = ev(vec.tensor_scalar(T.i2[:], T.pidx[:], 3, None, A.bitwise_and))
-    wait(vec, e1, e2)
+    wait("v", e1, e2)
     e_key = ev(vec.tensor_tensor(T.keyp[:], T.i1[:], T.i2[:], A.add))
     if rank == 0:
         e3 = ev(vec.tensor_scalar(T.i3[:], T.pidx[:], 12, None, A.bitwise_and))
-        wait(vec, e3, e_key)
+        wait("v", e3, e_key)
         e_k0 = ev(vec.tensor_scalar(T.key0[:], T.i3[:], 100.0, T.keyp[:, 0:1], A.mult, A.add))
     else:
         e_k0 = ev(vec.tensor_copy(T.key0[:], T.pidx[:]))
-        wait(vec, e_key)
-    wait(vec, e_km, e_m32)
-    e_sb = ev(vec.tensor_scalar(T.sb[:], T.km[:], T.keyp[:, 0:1], None, A.is_equal))
-    e_sf = ev(vec.tensor_scalar(T.sf[:], T.km[:], T.keyp[:, 0:1], None, A.is_equal))
-    e_so = ev(vec.tensor_scalar(T.so[:], T.m32[:], T.keyp[:, 0:1], None, A.is_equal))
-    wait(vec, e_k0)
-    consts = [e_sb, e_sf, e_so]
+        wait("v", e_key)
+    wait("v", e_km, e_m32)
+    consts = []
+
+    def const(ins):
+        ins.then_inc(T.sem["co"], 1)
+        consts.append(ins)
+
+    const(vec.tensor_scalar(T.sb[:], T.km[:], T.keyp[:, 0:1], None, A.is_equal))
+    const(vec.tensor_scalar(T.sf[:], T.km[:], T.keyp[:, 0:1], None, A.is_equal))
+    const(vec.tensor_scalar(T.so[:], T.m32[:], T.keyp[:, 0:1], None, A.is_equal))
+    e_one = ev(vec.memset(T.one[0:1, :], 1.0))
+    wait("v", e_hs)
+    e_hr = ev(vec.tensor_copy(T.hrf[0:1, :], T.hri[0:1, :]))
+    wait("t", e_one, e_hr)
+    e_ht = [ev(ten.matmul(T.pa0[:, k:k + 1], T.hrf[0:1, k:256:2], T.one[0:1, :], True, True)) for k in range(2)]
+    wait("v", e_k0)
     if rank == 0:
-        consts.append(ev(vec.tensor_scalar(T.ex[:, 0:128], T.km[:], T.key0[:, 0:1], None, A.is_equal)))
+        const(vec.tensor_scalar(T.ex[:, 0:128], T.km[:], T.key0[:, 0:1], None, A.is_equal))
         e_c = ev(vec.memset(T.cm[:], 0.0))
-        wait(vec, e_c)
+        wait("v", e_c)
         for b in range(4):
             o = 128 * b + 32 * b
-            consts.append(ev(vec.tensor_scalar(T.cm[:, o:o + 32], T.m32[:], T.key0[:, 0:1], None, A.is_equal)))
+            const(vec.tensor_scalar(T.cm[:, o:o + 32], T.m32[:], T.key0[:, 0:1], None, A.is_equal))
     else:
         for b in range(4):
-            consts.append(ev(vec.tensor_scalar(T.ex[:, 128 * b:128 * b + 128], T.km[:], float(32 * b), T.key0[:, 0:1],
-                                               A.add, A.is_equal)))
-    wait(ten, *consts)
+            const(vec.tensor_scalar(T.ex[:, 128 * b:128 * b + 128], T.km[:], float(32 * b), T.key0[:, 0:1],
+                                    A.add, A.is_equal))
+    wait("t", ("co", len(consts)))
 
-    wait(vec, e_hs)
-    e_hf = ev(vec.tensor_copy(T.hsf[:], T.hsi[:]))
-    wait(vec, e_hf)
+    wait("v", *e_ht)
+    e_hf = ev(vec.tensor_copy(T.hsf[:], T.pa0[:, 0:2]))
+    wait("v", e_hf)
+    wait("t", e_hf)
 
-    gathered = {}
+    came = {}
+    v0_piece = {}
+    for q in range(N):
+        for r, c0, c1, way in plan(q):
+            if r == rank:
+                for b in range(c0, c1):
+                    came[q, b] = ("ma%d_%d" % (q, c0), len(topo.engines(relay(q, r, way, T, topo), core)))
+                    if q == 0:
+                        v0_piece[b] = (c0, c1)
 
-    def hash_list(r):
-        wait(vec, e_ids if r == rank else arrived(r, "ida%d" % r))
-        a = ev(vec.tensor_scalar(slot(T.t1, r, L), slot(T.idl, r, L), T.hsf[:, 0:1], T.hsf[:, 1:2], A.mult, A.add))
-        wait(vec, a)
-        b = ev(vec.tensor_scalar(slot(T.t2, r, L), slot(T.t1, r, L), 4, 4095, A.logical_shift_right, A.bitwise_and))
-        wait(vec, b)
-        c = ev(vec.tensor_copy(slot(T.offs, r, L), slot(T.t2, r, L)))
-        wait(vec, c)
-        wait(act, c)
-        if r == rank:
-            wait(vec, e_mat)
-            wait(act, e_mat)
-
-    def gather(r, split):
-        gathered[r] = {}
-        for q, b0, b1 in split:
-            dst = T.gat[:, r * K + b0 * C:r * K + b1 * C]
-            src = T.win[:].indirect(T.offs[:, r * L + b0 * C // 16:r * L + b1 * C // 16])
-            e = ev(vec.tensor_copy(dst, src) if q == "v" else act.activation(dst, src, ActivationFunctionType.Copy))
-            for b in range(b0, b1):
-                gathered[r][b] = e
-
-    hash_list(rank)
-    gather(rank, HALF)
     PA = [T["pa%d" % b] for b in range(NC)]
     PB = [T["pb%d" % b] for b in range(NC)]
     left, right = slice(0, C), slice(C, 2 * C)
     col = [slice(b * C, (b + 1) * C) for b in range(NC)]
-    e_v0 = {}
-    if rank == 0:
-        for b in range(NC):
-            wait(ten, gathered[0][b])
-            e_v0[b] = ev(ten.matmul(PA[b][:, left], T.ex[:, 0:128], T.gat[:, col[b]], True, True))
-        copies, packed = [], []
+    hashed, gathered, part, packed, ready, e_v0, e_hi, e_mm, e_fin = {}, {}, {}, {}, {}, {}, {}, {}, {}
+    freed = {b: [] for b in range(NC)}
+    stored = []
 
-        def unload(i):
-            r = SERVE[0][i]
-            wait(vec, packed[i])
-            e = ev(vec.tensor_copy(slot(T.c0s, r, 256), PB[i][:, 0:256]))
-            copies.append(e)
-            wait(g, e)
-            send(r, T.c0l[:], slot(T.c0s, r, 256), "va")
+    def hash1(w):
+        s, n = hash_slot(rank, int(w[0])), len(w)
+        for r in map(int, w):
+            wait("v", e_ids if r == rank else ("ida%d" % r, len(topo.engines(T.cores[r], core))))
+        part[w] = ev(vec.tensor_scalar(slot(T.t1, s, L, n), slot(T.idl, s, L, n), T.hsf[:, 0:1], T.hsf[:, 1:2],
+                                       A.mult, A.add))
 
-        for i, r in enumerate(SERVE[0]):
-            hash_list(r)
-            gather(r, SPLIT[0])
-            ins = None
-            for b in range(NC):
-                wait(ten, gathered[r][b])
-                m = r * K + b * C
-                ins = ten.matmul(PB[i][:, 0:256], T.cm[:, 128 * b:128 * b + 128], T.gat[:, m:m + C], b == 0, b == NC - 1)
-            packed.append(ev(ins))
-            if i:
-                unload(i - 1)
-        unload(N - 2)
-        wait(ten, *copies)
-    else:
-        for r in SERVE[rank]:
-            hash_list(r)
-            gather(r, SPLIT[rank])
-        relays = relays_of(core, T, topo)
-        for i, (r, c0, c1, way) in enumerate(PLAN[rank]):
-            wait(g, *sorted(set(gathered[r][b] for b in range(c0, c1))))
-            m = slice(r * K + c0 * C, r * K + c1 * C)
-            if way < 0:
-                send(r, T.land[:, rank * K + c0 * C:rank * K + c1 * C], T.gat[:, m], "ma%d_%d" % (rank, c0))
-            else:
-                rid, pid, _se = topo.addr(relays[way])
-                eng = inner_engines(core, relays[way], T.cores[r], topo)
-                g.remote_dma(T.gat[:, m], T.gat[:, m], T.sem["rl%d" % i], T.sem["ls"], pid, rid, sum(1 << e for e in eng))
-                sent[0] += len(eng)
-        wait(ten, arrived(0, "va"))
-        for b in range(NC):
-            e_v0[b] = ev(ten.matmul(PA[b][:, left], T.ex[:, 128 * b:128 * b + 128], T.c0l[:], True, True))
+    def hash2(w):
+        s, n = hash_slot(rank, int(w[0])), len(w)
+        wait("v", part.pop(w))
+        part["y" + w] = ev(vec.tensor_scalar(slot(T.t2, s, L, n), slot(T.t1, s, L, n), 4, 4095,
+                                             A.logical_shift_right, A.bitwise_and))
 
-    came = {}
-    for q in PLAN:
-        for r, c0, c1, way in PLAN[q]:
-            if r == rank:
-                src = T.cores[q] if way < 0 else relays_of(T.cores[q], T, topo)[way]
-                for b in range(c0, c1):
-                    came[q, b] = ("ma%d_%d" % (q, c0), len(topo.engines(src, core)))
+    def hash3(w):
+        s, n = hash_slot(rank, int(w[0])), len(w)
+        wait("v", part.pop("y" + w))
+        e = ev(vec.tensor_copy(slot(T.offs, s, L, n), slot(T.t2, s, L, n)))
+        for r in map(int, w):
+            hashed[r] = e
 
-    def picks(s, b):
+    def hash_all(w):
+        hash1(w)
+        hash2(w)
+        hash3(w)
+
+    def copy(q, dst, src):
+        return ev(vec.tensor_copy(dst, src) if q == "v" else act.activation(dst, src, ActivationFunctionType.Copy))
+
+    def gather(q, w):
+        r, b0, b1 = map(int, w)
+        wait(q, hashed[r], e_mat)
+        o = hash_slot(rank, r) * L
+        e = copy(q, T.gat[:, r * K + b0 * C:r * K + b1 * C],
+                 T.win[:].indirect(T.offs[:, o + b0 * C // 16:o + b1 * C // 16]))
+        for b in range(b0, b1):
+            gathered[r, b] = e
+
+    def pack(w):
+        r, b0, b1 = map(int, w)
+        k, n = len(packed) % NC, (b1 - b0) * C // 4
+        assert len(freed[k]) == len(packed) // NC
+        wait("t", *freed[k])
+        for a in range(4):
+            m = b0 * C + a * n
+            wait("t", gathered[r, m // C], gathered[r, (m + n - 1) // C])
+            ins = ten.matmul(PB[k][:, 0:n], T.cm[:, 128 * a:128 * a + 128], T.gat[:, r * K + m:r * K + m + n],
+                             a == 0, a == 3)
+        packed[w] = (k, ev(ins))
+
+    def unload(q, w):
+        r, b0, b1 = map(int, w)
+        k, e = packed[w]
+        wait(q, e)
+        ready[r, b0] = copy(q, T.c0s[:, r * 256 + b0 * 64:r * 256 + b1 * 64], PB[k][:, 0:(b1 - b0) * 64])
+        freed[k].append(ready[r, b0])
+
+    def expand(b):
+        if rank == 0:
+            wait("t", gathered[0, b])
+            e_v0[b] = [ev(ten.matmul(PA[b][:, left], T.ex[:, 0:128], T.gat[:, col[b]], True, True))]
+            return
+        b0, b1 = v0_piece[b]
+        n = (b1 - b0) * C // 4
+        wait("t", came[0, b])
+        cuts = sorted(set(x for x in range(b * C, (b + 1) * C + 1) if x % C == 0 or (x - b0 * C) % n == 0))
+        e_v0[b] = []
+        for x0, x1 in zip(cuts, cuts[1:]):
+            a, o = divmod(x0 - b0 * C, n)
+            e_v0[b].append(ev(ten.matmul(PA[b][:, x0 - b * C:x1 - b * C], T.ex[:, 128 * a:128 * a + 128],
+                                         T.c0l[:, b0 * 64 + o:b0 * 64 + o + x1 - x0], True, True)))
+
+    def picks(s, b, j=None):
         m = s * K + b * C
+        m = slice(m, m + C) if j is None else slice(m + j, m + C, 2)
         if s == rank:
-            return T.gat[:, m:m + C], gathered[rank][b]
-        return T.land[:, m:m + C], came[s, b]
+            return T.gat[:, m], gathered[rank, b]
+        return T.land[:, m], came[s, b]
 
-    e_hi, e_mm, e_fin = {}, {}, {}
+    def bank(b):
+        assert len(freed[b]) == len([k for k in range(len(plan(0))) if rank == 0 and k % NC == b])
+        return freed[b]
 
     def m1(b):
         ap, e = picks(1, b)
-        wait(vec, e_v0[b], e)
-        if b in WHOLE[rank]:
+        wait("v", *e_v0[b], e)
+        if str(b) in WHOLE[rank]:
             e = ev(vec.tensor_tensor(T.p1[:, col[b]], PA[b][:, left], ap, A.mult))
-            wait(ten, e)
+            wait("t", e, *bank(b))
             e_mm[1, b] = ev(ten.matmul(PB[b][:, left], T.sf[:], T.p1[:, col[b]], True, True))
         else:
             e = ev(vec.tensor_tensor(PA[b][:, right], PA[b][:, left], ap, A.mult))
-            wait(act, e)
+            wait("s", e)
             e_hi[b] = ev(act.activation(T.hi[:, col[b]], PA[b][:, right], ActivationFunctionType.Copy))
 
     def lo(b):
-        wait(vec, e_hi[b])
+        wait("v", e_hi[b])
         e = ev(vec.tensor_tensor(T.lo[:, col[b]], PA[b][:, right], T.hi[:, col[b]], A.subtract))
-        wait(ten, e_hi[b])
+        wait("t", e_hi[b], *bank(b))
         ten.matmul(PB[b][:, left], T.sb[:], T.hi[:, col[b]], True, False)
-        wait(ten, e)
+        wait("t", e)
         e_mm[1, b] = ev(ten.matmul(PB[b][:, left], T.sb[:], T.lo[:, col[b]], False, True))
 
     def m2(b):
         ap, e = picks(2, b)
-        wait(vec, e_mm[1, b], e)
+        wait("v", e_mm[1, b], e)
         e = ev(vec.tensor_tensor(T.p2[:, col[b]], PB[b][:, left], ap, A.mult))
-        wait(ten, e)
+        wait("t", e)
         e_mm[2, b] = ev(ten.matmul(PB[b][:, right], T.sf[:], T.p2[:, col[b]], True, True))
 
     def m3(b):
         ap, e = picks(3, b)
-        wait(vec, e_mm[2, b], e)
+        wait("v", e_mm[2, b], e)
         e = ev(vec.tensor_tensor(T.p3[:, col[b]], PB[b][:, right], ap, A.mult))
-        wait(ten, e)
-        e_fin[b] = [ev(ten.matmul(PA[b][:, 32 * j:32 * j + 32], T.p3[:, b * C + j:(b + 1) * C:2], T.so[:], True, True))
-                    for j in range(2)]
+        wait("t", e)
+        e = [ev(ten.matmul(PA[b][:, 32 * j:32 * j + 32], T.p3[:, b * C + j:(b + 1) * C:2], T.so[:], True, True))
+             for j in range(2)]
+        for j in range(2):
+            e_fin[b, j] = (PA[b][:, 32 * j:32 * j + 32], e)
 
-    stored = []
+    halves = {}
+
+    def half(j, w):
+        s, b = map(int, w)
+        if (b, j) in halves:
+            done, to, e = halves[b, j]
+            assert done == s - 1
+            src, es = to[:, 0:C // 2], [e]
+        else:
+            assert j == 0 or (b, 0) in halves
+            was, o = ((PA[b], 0), (PB[b], 0), (PB[b], C))[s - 1]
+            src, es = was[:, o + j:o + C:2], e_v0[b] if s == 1 else [e_mm[s - 1, b]]
+            to = was if j else PB[b] if s == 1 else PA[b]
+        ap, e = picks(s, b, j)
+        wait("v", *es, e)
+        p = (T.p1, T.p2, T.p3)[s - 1][:, b * C + j * C // 2:b * C + (j + 1) * C // 2]
+        e = ev(vec.tensor_tensor(p, src, ap, A.mult))
+        wait("t", e, *bank(b))
+        if s < 3:
+            halves[b, j] = (s, to, ev(ten.matmul(to[:, 0:C // 2], T.sf[:], p, True, True)))
+        else:
+            halves[b, j] = (s, to, None)
+            e_fin[b, j] = (to[:, 0:32], [ev(ten.matmul(to[:, 0:32], p, T.so[:], True, True))])
 
     def out(b):
-        wait(vec, *e_fin[b])
+        queues = "y" if busy[0] else "ys"
         for j in range(2):
-            e = ev(vec.transpose(T.yb[:, 64 * b + j:64 * b + 64:2], PA[b][:, 32 * j:32 * j + 32]))
-            wait(sync, e)
-            wait(act, e)
+            ap, es = e_fin[b, j]
+            wait("v", *es)
+            e = ev(vec.transpose(T.yb[:, 64 * b + j:64 * b + 64:2], ap))
+            for q in queues:
+                wait(q, e)
         for a in range(4):
-            q = act if a % 2 else sync
             o = b * C + 64 * a
-            q.dma_start(T.y[:, o:o + 64], T.yb[32 * a:32 * a + 32, 64 * b:64 * b + 64]).then_inc(T.sem["st"], 16)
+            names[queues[a % len(queues)]].dma_start(
+                T.y[:, o:o + 64], T.yb[32 * a:32 * a + 32, 64 * b:64 * b + 64]).then_inc(T.sem["st"], 16)
             stored.append(16)
 
-    do = {"m1": m1, "lo": lo, "m2": m2, "m3": m3, "ou": out}
-    for step in ORDER[rank].split():
-        do[step[:2]](int(step[2]))
-    wait(sync, ("st", sum(stored)))
-    wait(g, ("ls", sent[0]))
+    two = {"m1": m1, "lo": lo, "m2": m2, "m3": m3, "ou": out}
+    one = {"h": hash_all, "x": hash1, "y": hash2, "z": hash3, "p": pack, "e": lambda w: expand(int(w)),
+           "v": lambda w: gather("v", w), "s": lambda w: gather("s", w),
+           "U": lambda w: unload("v", w), "u": lambda w: unload("s", w),
+           "A": lambda w: half(0, w), "B": lambda w: half(1, w)}
+    steps = PROG[rank].split()
+    busy = [True]
+    for i, step in enumerate(steps):
+        busy[0] = any(w[0] in "sul" for w in steps[i:])
+        if step[:2] in two:
+            two[step[:2]](int(step[2]))
+        else:
+            one[step[0]](step[1:])
+
+    for i, (r, c0, c1, way) in enumerate(plan(rank)):
+        dst = T.cores[r]
+        if rank == 0:
+            wait("g", ready[r, c0])
+            send(dst, T.c0l[:, c0 * 64:c1 * 64], T.c0s[:, r * 256 + c0 * 64:r * 256 + c1 * 64], "ma0_%d" % c0,
+                 topo.engines(core, dst))
+            continue
+        wait("g", *sorted(set(gathered[r, b] for b in range(c0, c1))))
+        src = T.gat[:, r * K + c0 * C:r * K + c1 * C]
+        if way == "d":
+            send(dst, T.land[:, rank * K + c0 * C:rank * K + c1 * C], src, "ma%d_%d" % (rank, c0), topo.engines(core, dst))
+        else:
+            send(relay(rank, r, way, T, topo), held(T, rank, r, c0, c1, way), src, "e%d" % (16 * rank + i),
+                 first_engines(rank, r, way, T, topo))
+    wait("y", ("st", sum(stored)))
+    wait("g", ("ls", sent[0]))

@@ -28,7 +28,6 @@ SCRATCH = {
     "p3": ("sbuf", [128, K], "float32"),
     "yb": ("sbuf", [128, NC * 64], "float32"),
     "km": ("sbuf", [128, 128], "float32"),
-    "m32": ("sbuf", [128, 32], "float32"),
     "pidx": ("sbuf", [128, 1], "int32"),
     "i1": ("sbuf", [128, 1], "int32"),
     "i2": ("sbuf", [128, 1], "int32"),
@@ -37,7 +36,6 @@ SCRATCH = {
     "key0": ("sbuf", [128, 1], "float32"),
     "sf": ("sbuf", [128, 128], "float32"),
     "sb": ("sbuf", [128, 128], "bfloat16"),
-    "so": ("sbuf", [128, 32], "float32"),
     "ex": ("sbuf", [128, 512], "bfloat16"),
     "cm": ("sbuf", [128, 512], "bfloat16"),
 }
@@ -45,7 +43,8 @@ for _b in range(NC):
     SCRATCH["pa%d" % _b] = ("psum", [128, 2 * C], "float32")
     SCRATCH["pb%d" % _b] = ("psum", [128, 2 * C], "float32")
 SEMAPHORES = (["e%d" % i for i in range(126)] + ["ida%d" % r for r in range(N)]
-              + ["ma%d_%d" % (q, b) for q in range(N) for b in range(NC)] + ["ls", "st", "co"])
+              + ["ma%d_%d" % (q, b) for q in range(N) for b in range(NC)] + ["ls", "st", "co", "wi"])
+WIDE = {0: 0}
 
 IDS_TO = {0: "132", 1: "023", 2: "301", 3: "210"}
 PLAN = {0: "102d 202d 302d 224d 324d 124d",
@@ -63,6 +62,8 @@ PROG = {0: "h0 v002 e0 s024 e2 e1 e3 h1 s102 h2 p102 h3 v302 s202 p202 u102 p302
         3: "h3 v302 s324 h2 s202 v234 h10 v223 s034 s003 v102 e0 v124 e1 "
            "A10 A11 B10 B11 A20 B20 A21 B21 A30 B30 A31 ou0 e2 e3 B31 A12 B12 m13 ou1 A22 B22 A23 B23 A32 B32 A33 B33 "
            "ou2 ou3"}
+_C = {'IDS_TO': {0: '231', 1: '320', 2: '013', 3: '102'}, 'PLAN': {0: '201d 301d 101d 234a 334b 134a 212d 312d 112d 223c 323d 123d', 1: '301d 201d 001d 334a 234b 034a 312d 212d 012d 323a 223d 023d', 2: '001d 101d 301d 034a 134b 334a 012d 112d 312d 023c 123d 323d', 3: '101d 001d 201d 134a 034b 234a 112d 012d 212d 023d 223d 123c'}, 'PROG': {0: 'h0 v012 v001 x2 s024 x3 y2 y3 z2 z3 s201 h1 s301 v101 s234 s334 v212 v134 e0 v312 s223 s112 A10 s323 s123 e3 e1 B10 A20 B20 A30 B30 A11 B11 ou0 A21 B21 m13 A12 B12 A31 B31 A23 B23 A22 B22 ou1 A33 B33 A32 B32 ou3 ou2', 1: 'x1 y1 z1 v102 x3 s124 x2 y3 y2 z3 z2 s301 h0 s201 v001 s334 s234 v034 s312 s012 s323 s023 s223 v212 A10 B10 A20 B20 A30 B30 A11 e3 B11 ou0 A21 B21 A12 B12 A13 A22 B13 B22 A23 A31 B23 B31 A32 B32 A33 B33 ou1 ou2 ou3', 2: 'h2 s202 s224 x0 x1 y0 y1 z0 z1 h3 s001 s101 s034 s134 v301 v334 s012 v112 s312 s023 s123 A10 B10 A20 B20 s323 A30 e1 B30 A11 B11 ou0 A21 B21 e3 A31 B31 A13 B13 A12 B12 A23 B23 A22 B22 ou1 A33 B33 A32 B32 ou3 ou2', 3: 'h3 s301 v312 s323 v334 x1 x0 y1 y0 z1 z0 s101 h2 s001 v201 s134 s034 v234 s112 v012 v123 s223 s023 m10 m20 A11 s212 B11 m30 A21 B21 e3 ou0 e2 A31 B31 A13 B13 m12 ou1 A23 B23 A22 B22 A33 B33 A32 B32 ou3 ou2'}, 'WHOLE': {0: '0123', 1: '0123', 2: '0123', 3: '0123'}, 'WIDE': {0: 1}}
+IDS_TO, PLAN, PROG, WHOLE, WIDE = _C["IDS_TO"], _C["PLAN"], _C["PROG"], _C["WHOLE"], _C["WIDE"]
 NEAR, FAR = "abcefg", "mnop"
 
 
@@ -101,7 +102,7 @@ def held(T, q, r, c0, c1, way):
 
 def relay_program(g, core, T, topo):
     sent = 0
-    for i, q in sorted((i, q) for q in range(1, N) for i in range(len(plan(q)))):
+    for i, q in sorted((i, q) for q in range(N) for i in range(len(plan(q)))):
         r, c0, c1, way = plan(q)[i]
         if relay(q, r, way, T, topo) != core:
             continue
@@ -151,60 +152,63 @@ def rank_program(g, core, T, topo):
     own = slot(T.idl, hash_slot(rank, rank), L)
     e_ids = ev(sync.dma_start(own, T.ids[:]), 16)
     e_hs = ev(act.dma_start(T.hri[0:1, :], T.hs[:]), 16)
-    e_mat = ev(sync.dma_start(T.win[:], T.mat[:]), 16)
+    if rank == 0 and WIDE[0]:
+        for p in range(16):
+            (act if p % 2 else sync).dma_start(T.win[p:128:16, :], T.mat[p // 4:128:16, :]).then_inc(T.sem["wi"], 16)
+        e_mat = ("wi", 256)
+    else:
+        e_mat = ev(sync.dma_start(T.win[:], T.mat[:]), 16)
 
     e_p = ev(g.iota(T.pidx[:], [[1, 1]], 0, 1))
     e_km = ev(g.iota(T.km[:], [[1, 32], [0, 4]], 0, 0, allow_small_or_imprecise_dtypes=True))
-    e_m32 = ev(g.iota(T.m32[:], [[1, 32]], 0, 0, allow_small_or_imprecise_dtypes=True))
     wait("g", e_ids)
     for r in map(int, IDS_TO[rank]):
         send(T.cores[r], slot(T.idl, hash_slot(r, rank), L), own, "ida%d" % rank, topo.engines(core, T.cores[r]))
 
+    e_one = ev(vec.memset(T.one[0:1, :], 1.0))
+    if rank == 0:
+        e_c = ev(vec.memset(T.cm[:], 0.0))
     wait("v", e_p)
     e1 = ev(vec.tensor_scalar(T.i1[:], T.pidx[:], 2, 28, A.logical_shift_right, A.bitwise_and))
     e2 = ev(vec.tensor_scalar(T.i2[:], T.pidx[:], 3, None, A.bitwise_and))
-    wait("v", e1, e2)
-    e_key = ev(vec.tensor_tensor(T.keyp[:], T.i1[:], T.i2[:], A.add))
     if rank == 0:
         e3 = ev(vec.tensor_scalar(T.i3[:], T.pidx[:], 12, None, A.bitwise_and))
-        wait("v", e3, e_key)
-        e_k0 = ev(vec.tensor_scalar(T.key0[:], T.i3[:], 100.0, T.keyp[:, 0:1], A.mult, A.add))
     else:
         e_k0 = ev(vec.tensor_copy(T.key0[:], T.pidx[:]))
-        wait("v", e_key)
-    wait("v", e_km, e_m32)
-    consts = []
+    wait("v", e1, e2)
+    e_key = ev(vec.tensor_tensor(T.keyp[:], T.i1[:], T.i2[:], A.add))
+    wait("v", e_key, e_km)
+    if rank == 0:
+        wait("v", e3)
+        e_k0 = ev(vec.tensor_scalar(T.key0[:], T.i3[:], 100.0, T.keyp[:, 0:1], A.mult, A.add))
+    e_sf = ev(vec.tensor_scalar(T.sf[:], T.km[:], T.keyp[:, 0:1], None, A.is_equal))
+    n_const = 5
 
     def const(ins):
         ins.then_inc(T.sem["co"], 1)
-        consts.append(ins)
 
-    const(vec.tensor_scalar(T.sb[:], T.km[:], T.keyp[:, 0:1], None, A.is_equal))
-    const(vec.tensor_scalar(T.sf[:], T.km[:], T.keyp[:, 0:1], None, A.is_equal))
-    const(vec.tensor_scalar(T.so[:], T.m32[:], T.keyp[:, 0:1], None, A.is_equal))
-    e_one = ev(vec.memset(T.one[0:1, :], 1.0))
-    wait("v", e_hs)
+    def ex_block(b):
+        const(vec.tensor_scalar(T.ex[:, 128 * b:128 * b + 128], T.km[:], float(32 * b), T.key0[:, 0:1],
+                                A.add, A.is_equal))
+
+    wait("s", e_sf)
+    const(act.activation(T.sb[:], T.sf[:], ActivationFunctionType.Copy))
+    wait("v", e_hs, e_k0)
     e_hr = ev(vec.tensor_copy(T.hrf[0:1, :], T.hri[0:1, :]))
     wait("t", e_one, e_hr)
     e_ht = [ev(ten.matmul(T.pa0[:, k:k + 1], T.hrf[0:1, k:256:2], T.one[0:1, :], True, True)) for k in range(2)]
-    wait("v", e_k0)
+    e_ex = ev(vec.tensor_scalar(T.ex[:, 0:128], T.km[:], T.key0[:, 0:1], None, A.is_equal))
     if rank == 0:
-        const(vec.tensor_scalar(T.ex[:, 0:128], T.km[:], T.key0[:, 0:1], None, A.is_equal))
-        e_c = ev(vec.memset(T.cm[:], 0.0))
-        wait("v", e_c)
+        wait("s", e_ex, e_c)
         for b in range(4):
-            o = 128 * b + 32 * b
-            const(vec.tensor_scalar(T.cm[:, o:o + 32], T.m32[:], T.key0[:, 0:1], None, A.is_equal))
+            const(act.activation(T.cm[:, 160 * b:160 * b + 32], T.ex[:, 0:128:4], ActivationFunctionType.Copy))
     else:
-        for b in range(4):
-            const(vec.tensor_scalar(T.ex[:, 128 * b:128 * b + 128], T.km[:], float(32 * b), T.key0[:, 0:1],
-                                    A.add, A.is_equal))
-    wait("t", ("co", len(consts)))
-
+        ex_block(1)
+        n_const = 4
     wait("v", *e_ht)
     e_hf = ev(vec.tensor_copy(T.hsf[:], T.pa0[:, 0:2]))
     wait("v", e_hf)
-    wait("t", e_hf)
+    wait("t", e_hf, e_sf, e_ex, ("co", n_const))
 
     came = {}
     v0_piece = {}
@@ -218,6 +222,7 @@ def rank_program(g, core, T, topo):
 
     PA = [T["pa%d" % b] for b in range(NC)]
     PB = [T["pb%d" % b] for b in range(NC)]
+    so = T.sf[:, 0:128:4]
     left, right = slice(0, C), slice(C, 2 * C)
     col = [slice(b * C, (b + 1) * C) for b in range(NC)]
     hashed, gathered, part, packed, ready, e_v0, e_hi, e_mm, e_fin = {}, {}, {}, {}, {}, {}, {}, {}, {}
@@ -241,6 +246,9 @@ def rank_program(g, core, T, topo):
         s, n = hash_slot(rank, int(w[0])), len(w)
         wait("v", part.pop("y" + w))
         e = ev(vec.tensor_copy(slot(T.offs, s, L, n), slot(T.t2, s, L, n)))
+        if rank and not hashed:
+            ex_block(2)
+            ex_block(3)
         for r in map(int, w):
             hashed[r] = e
 
@@ -281,6 +289,11 @@ def rank_program(g, core, T, topo):
         freed[k].append(ready[r, b0])
 
     def expand(b):
+        if WIDE[0]:
+            ap, e = picks(0, b)
+            wait("s", e_hf, e)
+            e_v0[b] = [copy("s", PA[b][:, left], ap)]
+            return
         if rank == 0:
             wait("t", gathered[0, b])
             e_v0[b] = [ev(ten.matmul(PA[b][:, left], T.ex[:, 0:128], T.gat[:, col[b]], True, True))]
@@ -303,18 +316,28 @@ def rank_program(g, core, T, topo):
         return T.land[:, m], came[s, b]
 
     def bank(b):
-        assert len(freed[b]) == len([k for k in range(len(plan(0))) if rank == 0 and k % NC == b])
+        assert WIDE[0] or len(freed[b]) == len([k for k in range(len(plan(0))) if rank == 0 and k % NC == b])
         return freed[b]
+
+    def v0_event(b):
+        if b in e_v0 or not WIDE[0]:
+            return e_v0[b]
+        assert "e%d" % b not in steps
+        return None
 
     def m1(b):
         ap, e = picks(1, b)
-        wait("v", *e_v0[b], e)
+        v0, es = PA[b][:, left], v0_event(b)
+        if es is None:
+            v0, e0 = picks(0, b)
+            es = [e0]
+        wait("v", *es, e)
         if str(b) in WHOLE[rank]:
-            e = ev(vec.tensor_tensor(T.p1[:, col[b]], PA[b][:, left], ap, A.mult))
+            e = ev(vec.tensor_tensor(T.p1[:, col[b]], v0, ap, A.mult))
             wait("t", e, *bank(b))
             e_mm[1, b] = ev(ten.matmul(PB[b][:, left], T.sf[:], T.p1[:, col[b]], True, True))
         else:
-            e = ev(vec.tensor_tensor(PA[b][:, right], PA[b][:, left], ap, A.mult))
+            e = ev(vec.tensor_tensor(PA[b][:, right], v0, ap, A.mult))
             wait("s", e)
             e_hi[b] = ev(act.activation(T.hi[:, col[b]], PA[b][:, right], ActivationFunctionType.Copy))
 
@@ -338,7 +361,7 @@ def rank_program(g, core, T, topo):
         wait("v", e_mm[2, b], e)
         e = ev(vec.tensor_tensor(T.p3[:, col[b]], PB[b][:, right], ap, A.mult))
         wait("t", e)
-        e = [ev(ten.matmul(PA[b][:, 32 * j:32 * j + 32], T.p3[:, b * C + j:(b + 1) * C:2], T.so[:], True, True))
+        e = [ev(ten.matmul(PA[b][:, 32 * j:32 * j + 32], T.p3[:, b * C + j:(b + 1) * C:2], so, True, True))
              for j in range(2)]
         for j in range(2):
             e_fin[b, j] = (PA[b][:, 32 * j:32 * j + 32], e)
@@ -354,8 +377,11 @@ def rank_program(g, core, T, topo):
         else:
             assert j == 0 or (b, 0) in halves
             was, o = ((PA[b], 0), (PB[b], 0), (PB[b], C))[s - 1]
-            src, es = was[:, o + j:o + C:2], e_v0[b] if s == 1 else [e_mm[s - 1, b]]
+            src, es = was[:, o + j:o + C:2], v0_event(b) if s == 1 else [e_mm[s - 1, b]]
             to = was if j else PB[b] if s == 1 else PA[b]
+            if es is None:
+                src, e = picks(0, b, j)
+                es = [e]
         ap, e = picks(s, b, j)
         wait("v", *es, e)
         p = (T.p1, T.p2, T.p3)[s - 1][:, b * C + j * C // 2:b * C + (j + 1) * C // 2]
@@ -365,7 +391,7 @@ def rank_program(g, core, T, topo):
             halves[b, j] = (s, to, ev(ten.matmul(to[:, 0:C // 2], T.sf[:], p, True, True)))
         else:
             halves[b, j] = (s, to, None)
-            e_fin[b, j] = (to[:, 0:32], [ev(ten.matmul(to[:, 0:32], p, T.so[:], True, True))])
+            e_fin[b, j] = (to[:, 0:32], [ev(ten.matmul(to[:, 0:32], p, so, True, True))])
 
     def out(b):
         queues = "y" if busy[0] else "ys"
@@ -389,7 +415,7 @@ def rank_program(g, core, T, topo):
     steps = PROG[rank].split()
     busy = [True]
     for i, step in enumerate(steps):
-        busy[0] = any(w[0] in "sul" for w in steps[i:])
+        busy[0] = any(w[0] in "sule" for w in steps[i:])
         if step[:2] in two:
             two[step[:2]](int(step[2]))
         else:
@@ -397,7 +423,7 @@ def rank_program(g, core, T, topo):
 
     for i, (r, c0, c1, way) in enumerate(plan(rank)):
         dst = T.cores[r]
-        if rank == 0:
+        if rank == 0 and not WIDE[0]:
             wait("g", ready[r, c0])
             send(dst, T.c0l[:, c0 * 64:c1 * 64], T.c0s[:, r * 256 + c0 * 64:r * 256 + c1 * 64], "ma0_%d" % c0,
                  topo.engines(core, dst))

@@ -1,14 +1,19 @@
+from concourse.bass import DstId, RemoteDMATransfer
 from concourse.mybir import AluOpType, ActivationFunctionType
 
 N = 4
 K = 1024
-C = 256
-NC = K // C
+U = 128
 L = K // 16
 A = AluOpType
+COPY = ActivationFunctionType.Copy
 
 SCRATCH = {
-    "idl": ("sbuf", [128, N * L], "int32"),
+    "idw": ("sbuf", [128, N * L], "int32"),
+    "hi": ("sbuf", [128, K], "bfloat16"),
+    "lo": ("sbuf", [128, K], "bfloat16"),
+    "sb": ("sbuf", [128, 128], "bfloat16"),
+    "idl": ("sbuf", [128, N * L], "uint16"),
     "hri": ("sbuf", [128, 256], "int32"),
     "hrf": ("sbuf", [128, 256], "float32"),
     "one": ("sbuf", [128, 1], "float32"),
@@ -19,101 +24,145 @@ SCRATCH = {
     "offs": ("sbuf", [128, N * L], "uint16"),
     "gat": ("sbuf", [128, N * K], "bfloat16"),
     "land": ("sbuf", [128, N * K], "bfloat16"),
-    "c0s": ("sbuf", [128, N * 256], "bfloat16"),
-    "c0l": ("sbuf", [128, 256], "bfloat16"),
-    "hi": ("sbuf", [128, K], "bfloat16"),
-    "lo": ("sbuf", [128, K], "bfloat16"),
     "p1": ("sbuf", [128, K], "float32"),
     "p2": ("sbuf", [128, K], "float32"),
     "p3": ("sbuf", [128, K], "float32"),
-    "yb": ("sbuf", [128, NC * 64], "float32"),
+    "yb": ("sbuf", [128, K // 4], "float32"),
     "km": ("sbuf", [128, 128], "float32"),
+    "kd": ("sbuf", [128, 128], "float32"),
     "pidx": ("sbuf", [128, 1], "int32"),
     "i1": ("sbuf", [128, 1], "int32"),
     "i2": ("sbuf", [128, 1], "int32"),
-    "i3": ("sbuf", [128, 1], "int32"),
     "keyp": ("sbuf", [128, 1], "float32"),
-    "key0": ("sbuf", [128, 1], "float32"),
     "sf": ("sbuf", [128, 128], "float32"),
-    "sb": ("sbuf", [128, 128], "bfloat16"),
-    "ex": ("sbuf", [128, 512], "bfloat16"),
-    "cm": ("sbuf", [128, 512], "bfloat16"),
+    "eye": ("sbuf", [128, 128], "bfloat16"),
 }
-for _b in range(NC):
-    SCRATCH["pa%d" % _b] = ("psum", [128, 2 * C], "float32")
-    SCRATCH["pb%d" % _b] = ("psum", [128, 2 * C], "float32")
-SEMAPHORES = (["e%d" % i for i in range(126)] + ["ida%d" % r for r in range(N)]
-              + ["ma%d_%d" % (q, b) for q in range(N) for b in range(NC)] + ["ls", "st", "co", "wi"])
-WIDE = {0: 0}
+for _b in range(K // U):
+    SCRATCH["pu%d" % _b] = ("psum", [128, 512], "float32")
+SEMAPHORES = (["e%d" % i for i in range(125)] + ["ida%d" % r for r in range(N)]
+              + ["ma%d_%d" % (q, b) for q in range(N) for b in range(4)] + ["ls", "st", "wi", "idr", "idb"])
 
-IDS_TO = {0: "132", 1: "023", 2: "301", 3: "210"}
-PLAN = {0: "102d 202d 302d 224d 324d 124d",
-        1: "002d 024a 302d 202d 324b 224d",
-        2: "302d 324a 002d 102d 024b 124d",
-        3: "202d 224a 102d 002d 124b 024d"}
-WHOLE = {0: "23", 1: "0123", 2: "123", 3: "0123"}
-PROG = {0: "h0 v002 e0 s024 e2 e1 e3 h1 s102 h2 p102 h3 v302 s202 p202 u102 p302 s124 U202 U302 v223 v234 p124 s324 "
-           "U124 p224 u224 p324 u324 "
-           "m10 m11 lo0 lo1 A20 A21 B20 B21 A30 B30 A12 B31 B12 A31 m13 A22 B22 m23 A32 ou1 ou0 B32 A33 B33 ou2 ou3",
-        1: "h1 v102 s124 h0 s002 s023 v034 h32 v302 s202 e0 s324 s234 e1 m11 m10 s223 "
-           "m21 A20 B20 A31 B31 A30 B30 ou1 ou0 e2 e3 A12 A13 B12 A22 B13 B22 B23 A23 A32 B33 B32 A33 ou2 ou3",
-        2: "h2 h3 v202 s224 s302 x1 x0 y0 y1 z0 s324 z1 v002 s102 e1 s123 s024 e0 s134 "
-           "A11 B11 m10 A21 B21 lo0 A31 B31 ou1 e2 e3 A12 B12 m13 m20 A22 B22 A23 B23 A30 B30 A32 B32 A33 B33 ou0 ou2 ou3",
-        3: "h3 v302 s324 h2 s202 v234 h10 v223 s034 s003 v102 e0 v124 e1 "
-           "A10 A11 B10 B11 A20 B20 A21 B21 A30 B30 A31 ou0 e2 e3 B31 A12 B12 m13 ou1 A22 B22 A23 B23 A32 B32 A33 B33 "
-           "ou2 ou3"}
-_C = {'IDS_TO': {0: '231', 1: '320', 2: '013', 3: '102'}, 'PLAN': {0: '201d 301d 101d 234a 334b 134a 212d 312d 112d 223c 323d 123d', 1: '301d 201d 001d 334a 234b 034a 312d 212d 012d 323a 223d 023d', 2: '001d 101d 301d 034a 134b 334a 012d 112d 312d 023c 123d 323d', 3: '101d 001d 201d 134a 034b 234a 112d 012d 212d 023d 223d 123c'}, 'PROG': {0: 'h0 v012 v001 x2 s024 x3 y2 y3 z2 z3 s201 h1 s301 v101 s234 s334 v212 v134 e0 v312 s223 s112 A10 s323 s123 e3 e1 B10 A20 B20 A30 B30 A11 B11 ou0 A21 B21 m13 A12 B12 A31 B31 A23 B23 A22 B22 ou1 A33 B33 A32 B32 ou3 ou2', 1: 'x1 y1 z1 v102 x3 s124 x2 y3 y2 z3 z2 s301 h0 s201 v001 s334 s234 v034 s312 s012 s323 s023 s223 v212 A10 B10 A20 B20 A30 B30 A11 e3 B11 ou0 A21 B21 A12 B12 A13 A22 B13 B22 A23 A31 B23 B31 A32 B32 A33 B33 ou1 ou2 ou3', 2: 'h2 s202 s224 x0 x1 y0 y1 z0 z1 h3 s001 s101 s034 s134 v301 v334 s012 v112 s312 s023 s123 A10 B10 A20 B20 s323 A30 e1 B30 A11 B11 ou0 A21 B21 e3 A31 B31 A13 B13 A12 B12 A23 B23 A22 B22 ou1 A33 B33 A32 B32 ou3 ou2', 3: 'h3 s301 v312 s323 v334 x1 x0 y1 y0 z1 z0 s101 h2 s001 v201 s134 s034 v234 s112 v012 v123 s223 s023 m10 m20 A11 s212 B11 m30 A21 B21 e3 ou0 e2 A31 B31 A13 B13 m12 ou1 A23 B23 A22 B22 A33 B33 A32 B32 ou3 ou2'}, 'WHOLE': {0: '0123', 1: '0123', 2: '0123', 3: '0123'}, 'WIDE': {0: 1}}
-IDS_TO, PLAN, PROG, WHOLE, WIDE = _C["IDS_TO"], _C["PLAN"], _C["PROG"], _C["WHOLE"], _C["WIDE"]
-NEAR, FAR = "abcefg", "mnop"
+CUTS = [0, 2, 4, 6, 8]
+LATE = [16]
+LATE_BY = ["abc"]
+LENDER = [3, 3, 0, 0, 0]
+NARROW = [0]
+ID_CALLS = ["01 l 2"]
+IDS_TO = {0: '231', 1: '320', 2: '013', 3: '102'}
+PLAN = {0: '201d 301d 101d 223a 323a 123a 112d 312d 212d 234a 334d 134d',
+        1: '301d 201d 001d 323a 223a 023a 012d 212d 312d 334a 234d 034d',
+        2: '001d 101d 301d 023a 123a 323a 312d 112d 012d 034a 134d 334d',
+        3: '101d 001d 201d 123a 023a 223a 212d 012d 112d 134a 034d 234d'}
+PROG = {0: 'h0 v002 s024 t00 t01 t02 t03 x2 x3 y2 y3 z2 z3 s201 h1 v301 s101 v223 s323 v123 s112 v312 s212 hl s234 s334 s134 A10 B10 A20 B20 A11 A30 B11 B30 A21 B21 o0 A12 A31 B12 B31 A22 B22 o1 A13 A32 B13 B32 A23 B23 o2 A33 B33 o3',
+        1: 'h1 v102 s124 t10 t11 t12 t13 x3 x2 y3 y2 z3 z2 s301 h0 v201 s001 v323 s223 v023 s012 v212 s312 hl s334 s234 s034 A10 B10 A20 B20 A11 A30 B11 B30 A21 B21 o0 A12 A31 B12 B31 A22 B22 o1 A13 A32 B13 B32 A23 B23 o2 A33 B33 o3',
+        2: 'h2 v202 s224 x0 x1 y0 y1 z0 z1 s001 h3 v101 s301 v023 s123 v323 s312 v112 s012 hl s034 s134 s334 A10 B10 A20 B20 e01 A11 A30 B11 B30 A21 B21 e02 o0 A12 A31 B12 B31 A22 B22 e03 o1 A13 A32 B13 B32 A23 B23 o2 A33 B33 o3',
+        3: 'h3 v302 s324 x1 x0 y1 y0 z1 z0 s101 h2 v001 s201 v123 s023 v223 s212 v012 s112 hl s134 s034 s234 A10 B10 A20 B20 e01 A11 A30 B11 B30 A21 B21 e02 o0 A12 A31 B12 B31 A22 B22 e03 o1 A13 A32 B13 B32 A23 B23 o2 A33 B33 o3'}
+OTHER, OWN = "abe", "cfg"
 
 
 def plan(q):
     return [(int(w[0]), int(w[1]), int(w[2]), w[3]) for w in PLAN[q].split()]
 
 
-def hash_slot(q, r):
-    return "".join(w[1:] for w in PROG[q].split() if w[0] in "hx").index(str(r))
+def rounds(q, spec):
+    return " ".join("%s%d%d%s" % (r, b, b + 1, way) for b, ways, turned in spec
+                    for r, way in zip(IDS_TO[q][::-1] if turned else IDS_TO[q], ways))
 
 
-def relay(q, r, way, T, topo):
-    src, dst = T.cores[q], T.cores[r]
+def rule(q, on_vector, lag, stager="e", paired=""):
+    nc = len(CUTS) - 1
+    h = (nc + 1) // 2
+    p = ["h%d" % q, "v%d0%d" % (q, h), "s%d%d%d" % (q, h, nc)]
+    if q < 2:
+        p += ["t%d%d" % (q, b) for b in range(nc)]
+    p += [x + r for x in "xyz" for r in IDS_TO[q][:2]]
+    for k, (r, c0, c1, way) in enumerate(plan(q)):
+        if k == 1:
+            p.append("h" + IDS_TO[q][2])
+        if LATE[0] and "hl" not in p and CUTS[c0] * U // 16 >= L - LATE[0]:
+            p.append("hl")
+        p.append("%s%d%d%d" % ("v" if k in on_vector else "s", r, c0, c1))
+    w = []
+    for b in range(nc):
+        if q >= 2 and b:
+            w.append((lag * b + .3, stager + "0%d" % b))
+        for s in (1, 2, 3):
+            t = lag * b + s - (s == 1 and str(b) in paired) * .6
+            w += [(t + j * .01, "ABCD"[j] + "%d%d" % (s, b)) for j in range(CUTS[b + 1] - CUTS[b])]
+        if str(b) in paired:
+            w += [(lag * b + 1.2 + j * .01, "abcd"[j] + "1%d" % b) for j in range(CUTS[b + 1] - CUTS[b])]
+        w.append((lag * b + 4.5, "o%d" % b))
+    return " ".join(p + [x for _, x in sorted(w)])
+
+
+def named(q, text):
+    return text.translate(str.maketrans("wpqr", str(q) + IDS_TO[q]))
+
+
+PLANS = ['p01d q01d p12b+ r01d q12d r12d+ p23b q23a+ r23d q34a+ p34d r34d', 'q01d p01d r01d q12d p12b r12d p23a q23a+ r23d r34d q34b p34d']
+PROGS = ['xw yw zw vw02 tw0 tw1 sw24 xp tw2 tw3 xq yp yq xr zp zq yr zr vq01 vp12 sp01 sr01 vq23 sp23 vr12 xl sq12 yl zl sr23 sq34 vp34 sr34 A10 B10 A20 B20 B11 A11 A30 B30 A12 B21 B12 A21 B31 A22 A13 B13 B22 A23 B23 A31 B32 o0 A32 A33 B33 o1 o2 o3', 'hw xp sw24 xq yp xr yq sw02 zp yr sp01 zq vq01 zr vp12 vr01 vq23 vr12 sr23 sq12 xl yl zl sp23 sr34 vq34 sp34 t00 A10 B10 A20 B20 A11 B11 A30 B30 A21 B21 A12 B12 B31 A31 A22 A13 B13 B22 A23 B23 o1 B32 A32 A33 B33 o0 o2 o3']
+
+
+def spell():
+    for q in range(N):
+        PLAN[q], PROG[q] = named(q, PLANS[q // 2]), named(q, PROGS[q // 2])
+
+
+spell()
+
+
+def id_col(q, r, c):
+    if r == q:
+        return c
+    s = "".join(w[1:] for w in PROG[q].split() if w[0] in "hx" and w[1:] not in ("l", str(q))).index(str(r))
+    early = L - LATE[0]
+    return L + s * early + c if c < early else L + (N - 1) * early + s * LATE[0] + c - early
+
+
+def relay(q, way, T, topo):
+    src = T.cores[q]
     if way == "d":
         return src
-    if way in NEAR:
-        c = [x for x in topo.cores_of(src) if x != src]
-        c.sort(key=lambda x: (not all(topo.may_write(x, d) for d in T.cores), topo.die(x) == topo.die(src)))
-        return c[NEAR.index(way)]
-    c = [x for x in range(topo.CHIPS * topo.CORES_PER_CHIP)
-         if topo.mates(topo.chip(x), topo.chip(dst)) and topo.may_write(x, dst)]
-    c.sort(key=lambda x: topo.die(x) == topo.die(dst))
-    return c[FAR.index(way)]
+    c = [x for x in topo.cores_of(src) if x != src and (topo.die(x) == topo.die(src)) == (way in OWN)]
+    c.sort(key=lambda x: not all(topo.may_write(x, d) for d in T.cores))
+    return c[(OWN if way in OWN else OTHER).index(way)]
 
 
 def first_engines(q, r, way, T, topo):
-    src, via = T.cores[q], relay(q, r, way, T, topo)
-    eng = topo.engines(src, via)
-    return [e for e in eng if e not in topo.engines(src, T.cores[r])] if way in NEAR else eng
+    src = T.cores[q]
+    return [e for e in topo.engines(src, relay(q, way, T, topo)) if e not in topo.engines(src, T.cores[r])]
 
 
-def held(T, q, r, c0, c1, way):
-    buf, s = (T.gat, r) if way in NEAR else (T.land, q)
-    return buf[:, s * K + c0 * C:s * K + c1 * C]
+def ids_engines(q, r, T, topo):
+    eng = topo.engines(T.cores[q], T.cores[r])
+    return [eng[0::2], eng[1::2], eng][IDS_TO[q].index(str(r))]
+
+
+def cols(buf, s, c0, c1):
+    return buf[:, s * K + CUTS[c0] * U:s * K + CUTS[c1] * U]
 
 
 def relay_program(g, core, T, topo):
-    sent = 0
-    for i, q in sorted((i, q) for q in range(N) for i in range(len(plan(q)))):
-        r, c0, c1, way = plan(q)[i]
-        if relay(q, r, way, T, topo) != core:
-            continue
-        dst = T.cores[r]
-        rid, pid, _se = topo.addr(dst)
-        g.wait_ge(T.sem["e%d" % (16 * q + i)], len(first_engines(q, r, way, T, topo)))
-        g.remote_dma(T.land[:, q * K + c0 * C:q * K + c1 * C], held(T, q, r, c0, c1, way),
-                     T.sem["ma%d_%d" % (q, c0)], T.sem["ls"], pid, rid, topo.mask(core, dst))
-        sent += len(topo.engines(core, dst))
-    if sent:
-        g.wait_ge(T.sem["ls"], sent)
+    sent = [0]
+
+    def send(r, out_ap, in_ap, sem):
+        rid, pid, _se = topo.addr(T.cores[r])
+        g.remote_dma(out_ap, in_ap, T.sem[sem], T.sem["ls"], pid, rid, topo.mask(core, T.cores[r]))
+        sent[0] += len(topo.engines(core, T.cores[r]))
+
+    for q in range(N):
+        for r, way in zip(map(int, IDS_TO[q]), LATE_BY[0]):
+            if LATE[0] and relay(q, way, T, topo) == core:
+                g.wait_ge(T.sem["idr"], len(first_engines(q, r, way, T, topo)))
+                o = id_col(r, q, L - LATE[0])
+                idl = T.idl if NARROW[0] else T.idw
+                send(r, idl[:, o:o + LATE[0]], idl[:, L - LATE[0]:L], "idb")
+        for i, (r, c0, c1, way) in enumerate(plan(q)):
+            if relay(q, way, T, topo) == core:
+                g.wait_ge(T.sem["e%d" % i], len(first_engines(q, r, way, T, topo)))
+                send(r, cols(T.land, q, c0, c1), cols(T.gat, r, c0, c1), "ma%d_%d" % (q, c0))
+    if sent[0]:
+        g.wait_ge(T.sem["ls"], sent[0])
 
 
 def rank_program(g, core, T, topo):
@@ -146,13 +195,12 @@ def rank_program(g, core, T, topo):
         g.remote_dma(out_ap, in_ap, T.sem[sem], T.sem["ls"], pid, rid, sum(1 << e for e in eng))
         sent[0] += len(eng)
 
-    def slot(buf, r, w, n=1):
-        return buf[:, r * w:(r + n) * w]
-
-    own = slot(T.idl, hash_slot(rank, rank), L)
-    e_ids = ev(sync.dma_start(own, T.ids[:]), 16)
+    steps = PROG[rank].split()
+    early = L - LATE[0]
+    idl = T.idl if NARROW[0] else T.idw
+    e_ld = ev(sync.dma_start(T.idw[:, 0:L], T.ids[:]), 16)
     e_hs = ev(act.dma_start(T.hri[0:1, :], T.hs[:]), 16)
-    if rank == 0 and WIDE[0]:
+    if rank == 0:
         for p in range(16):
             (act if p % 2 else sync).dma_start(T.win[p:128:16, :], T.mat[p // 4:128:16, :]).then_inc(T.sem["wi"], 16)
         e_mat = ("wi", 256)
@@ -161,95 +209,88 @@ def rank_program(g, core, T, topo):
 
     e_p = ev(g.iota(T.pidx[:], [[1, 1]], 0, 1))
     e_km = ev(g.iota(T.km[:], [[1, 32], [0, 4]], 0, 0, allow_small_or_imprecise_dtypes=True))
-    wait("g", e_ids)
-    for r in map(int, IDS_TO[rank]):
-        send(T.cores[r], slot(T.idl, hash_slot(r, rank), L), own, "ida%d" % rank, topo.engines(core, T.cores[r]))
-
+    if any(w[0] == "t" for w in steps):
+        e_kd = ev(g.iota(T.kd[:], [[1, 128]], 0, -1, allow_small_or_imprecise_dtypes=True))
     e_one = ev(vec.memset(T.one[0:1, :], 1.0))
-    if rank == 0:
-        e_c = ev(vec.memset(T.cm[:], 0.0))
     wait("v", e_p)
     e1 = ev(vec.tensor_scalar(T.i1[:], T.pidx[:], 2, 28, A.logical_shift_right, A.bitwise_and))
     e2 = ev(vec.tensor_scalar(T.i2[:], T.pidx[:], 3, None, A.bitwise_and))
-    if rank == 0:
-        e3 = ev(vec.tensor_scalar(T.i3[:], T.pidx[:], 12, None, A.bitwise_and))
-    else:
-        e_k0 = ev(vec.tensor_copy(T.key0[:], T.pidx[:]))
     wait("v", e1, e2)
     e_key = ev(vec.tensor_tensor(T.keyp[:], T.i1[:], T.i2[:], A.add))
-    wait("v", e_key, e_km)
-    if rank == 0:
-        wait("v", e3)
-        e_k0 = ev(vec.tensor_scalar(T.key0[:], T.i3[:], 100.0, T.keyp[:, 0:1], A.mult, A.add))
-    e_sf = ev(vec.tensor_scalar(T.sf[:], T.km[:], T.keyp[:, 0:1], None, A.is_equal))
-    n_const = 5
 
-    def const(ins):
-        ins.then_inc(T.sem["co"], 1)
+    e_ids = e_ld
+    if NARROW[0]:
+        wait("v", e_ld)
+        e_ids = ev(vec.tensor_copy(T.idl[:, 0:L], T.idw[:, 0:L]))
+    wait("g", e_ids)
+    to = [int(r) for r in IDS_TO[rank]]
 
-    def ex_block(b):
-        const(vec.tensor_scalar(T.ex[:, 128 * b:128 * b + 128], T.km[:], float(32 * b), T.key0[:, 0:1],
-                                A.add, A.is_equal))
+    def transfer(cores, outs, src, sem, eng):
+        sent[0] += len(eng)
+        return RemoteDMATransfer(dst_ids=[DstId(rid=topo.addr(c)[0], pnc=topo.addr(c)[1]) for c in cores],
+                                 dma_engine_mask=sum(1 << e for e in eng), remote_sem=T.sem[sem], srcs=[src], dsts=outs)
 
-    wait("s", e_sf)
-    const(act.activation(T.sb[:], T.sf[:], ActivationFunctionType.Copy))
-    wait("v", e_hs, e_k0)
+    tr = {}
+    if LATE[0]:
+        via = [relay(rank, way, T, topo) for way in sorted(set(LATE_BY[0]))]
+        tr["l"] = transfer(via, [idl[:, early:L]] * len(via), idl[:, early:L], "idr",
+                           first_engines(rank, to[0], LATE_BY[0][0], T, topo))
+    for k, r in enumerate(to):
+        o = id_col(r, rank, 0)
+        tr[str(k)] = transfer([T.cores[r]], [idl[:, o:o + early]], idl[:, 0:early], "ida%d" % rank,
+                              ids_engines(rank, r, T, topo))
+    for call in ID_CALLS[0].split():
+        if call[0] in tr:
+            g.remote_dma_fused([tr[k] for k in call], local_sem=T.sem["ls"])
+
+    PU = [T["pu%d" % u] for u in range(K // U)]
+    wait("v", e_hs)
     e_hr = ev(vec.tensor_copy(T.hrf[0:1, :], T.hri[0:1, :]))
     wait("t", e_one, e_hr)
-    e_ht = [ev(ten.matmul(T.pa0[:, k:k + 1], T.hrf[0:1, k:256:2], T.one[0:1, :], True, True)) for k in range(2)]
-    e_ex = ev(vec.tensor_scalar(T.ex[:, 0:128], T.km[:], T.key0[:, 0:1], None, A.is_equal))
-    if rank == 0:
-        wait("s", e_ex, e_c)
-        for b in range(4):
-            const(act.activation(T.cm[:, 160 * b:160 * b + 32], T.ex[:, 0:128:4], ActivationFunctionType.Copy))
-    else:
-        ex_block(1)
-        n_const = 4
+    e_ht = [ev(ten.matmul(PU[0][:, k:k + 1], T.hrf[0:1, k:256:2], T.one[0:1, :], True, True)) for k in range(2)]
+    wait("v", e_key, e_km)
+    e_sf = ev(vec.tensor_scalar(T.sf[:], T.km[:], T.keyp[:, 0:1], None, A.is_equal))
     wait("v", *e_ht)
-    e_hf = ev(vec.tensor_copy(T.hsf[:], T.pa0[:, 0:2]))
+    e_hf = ev(vec.tensor_copy(T.hsf[:], PU[0][:, 0:2]))
+    if any(w[0] == "t" for w in steps):
+        wait("v", e_kd)
+        wait("t", ev(vec.tensor_scalar(T.eye[:], T.kd[:], 0.0, None, A.is_equal)))
     wait("v", e_hf)
-    wait("t", e_hf, e_sf, e_ex, ("co", n_const))
+    wait("t", e_hf, e_sf)
 
     came = {}
-    v0_piece = {}
     for q in range(N):
         for r, c0, c1, way in plan(q):
             if r == rank:
                 for b in range(c0, c1):
-                    came[q, b] = ("ma%d_%d" % (q, c0), len(topo.engines(relay(q, r, way, T, topo), core)))
-                    if q == 0:
-                        v0_piece[b] = (c0, c1)
+                    came[q, b] = ("ma%d_%d" % (q, c0), len(topo.engines(relay(q, way, T, topo), core)))
 
-    PA = [T["pa%d" % b] for b in range(NC)]
-    PB = [T["pb%d" % b] for b in range(NC)]
     so = T.sf[:, 0:128:4]
-    left, right = slice(0, C), slice(C, 2 * C)
-    col = [slice(b * C, (b + 1) * C) for b in range(NC)]
-    hashed, gathered, part, packed, ready, e_v0, e_hi, e_mm, e_fin = {}, {}, {}, {}, {}, {}, {}, {}, {}
-    freed = {b: [] for b in range(NC)}
+    hashed, gathered, part, state = {}, {}, {}, {}
     stored = []
 
+    def span(w):
+        if w == "l":
+            return slice(N * L - (N - 1) * LATE[0], N * L)
+        o = id_col(rank, int(w[0]), 0)
+        return slice(o, o + (L if int(w[0]) == rank else early * len(w)))
+
     def hash1(w):
-        s, n = hash_slot(rank, int(w[0])), len(w)
-        for r in map(int, w):
-            wait("v", e_ids if r == rank else ("ida%d" % r, len(topo.engines(T.cores[r], core))))
-        part[w] = ev(vec.tensor_scalar(slot(T.t1, s, L, n), slot(T.idl, s, L, n), T.hsf[:, 0:1], T.hsf[:, 1:2],
-                                       A.mult, A.add))
+        if w == "l":
+            wait("v", ("idb", sum(len(topo.engines(T.cores[r], core)) for r in to)))
+        else:
+            wait("v", *[e_ids if r == rank else ("ida%d" % r, len(ids_engines(r, rank, T, topo))) for r in map(int, w)])
+        part[w] = ev(vec.tensor_scalar(T.t1[:, span(w)], idl[:, span(w)], T.hsf[:, 0:1], T.hsf[:, 1:2], A.mult, A.add))
 
     def hash2(w):
-        s, n = hash_slot(rank, int(w[0])), len(w)
         wait("v", part.pop(w))
-        part["y" + w] = ev(vec.tensor_scalar(slot(T.t2, s, L, n), slot(T.t1, s, L, n), 4, 4095,
+        part["y" + w] = ev(vec.tensor_scalar(T.t2[:, span(w)], T.t1[:, span(w)], 4, 4095,
                                              A.logical_shift_right, A.bitwise_and))
 
     def hash3(w):
-        s, n = hash_slot(rank, int(w[0])), len(w)
         wait("v", part.pop("y" + w))
-        e = ev(vec.tensor_copy(slot(T.offs, s, L, n), slot(T.t2, s, L, n)))
-        if rank and not hashed:
-            ex_block(2)
-            ex_block(3)
-        for r in map(int, w):
+        e = ev(vec.tensor_copy(T.offs[:, span(w)], T.t2[:, span(w)]))
+        for r in w:
             hashed[r] = e
 
     def hash_all(w):
@@ -257,183 +298,126 @@ def rank_program(g, core, T, topo):
         hash2(w)
         hash3(w)
 
-    def copy(q, dst, src):
-        return ev(vec.tensor_copy(dst, src) if q == "v" else act.activation(dst, src, ActivationFunctionType.Copy))
-
     def gather(q, w):
         r, b0, b1 = map(int, w)
-        wait(q, hashed[r], e_mat)
-        o = hash_slot(rank, r) * L
-        e = copy(q, T.gat[:, r * K + b0 * C:r * K + b1 * C],
-                 T.win[:].indirect(T.offs[:, o + b0 * C // 16:o + b1 * C // 16]))
+        c0, c1 = CUTS[b0] * U // 16, CUTS[b1] * U // 16
+        assert r == rank or c0 >= early or c1 <= early
+        wait(q, hashed[w[0] if r == rank or c0 < early else "l"], e_mat)
+        o = id_col(rank, r, c0)
+        src, dst = T.win[:].indirect(T.offs[:, o:o + c1 - c0]), cols(T.gat, r, b0, b1)
+        e = ev(vec.tensor_copy(dst, src) if q == "v" else act.activation(dst, src, COPY))
         for b in range(b0, b1):
             gathered[r, b] = e
 
-    def pack(w):
-        r, b0, b1 = map(int, w)
-        k, n = len(packed) % NC, (b1 - b0) * C // 4
-        assert len(freed[k]) == len(packed) // NC
-        wait("t", *freed[k])
-        for a in range(4):
-            m = b0 * C + a * n
-            wait("t", gathered[r, m // C], gathered[r, (m + n - 1) // C])
-            ins = ten.matmul(PB[k][:, 0:n], T.cm[:, 128 * a:128 * a + 128], T.gat[:, r * K + m:r * K + m + n],
-                             a == 0, a == 3)
-        packed[w] = (k, ev(ins))
+    def blocks(b):
+        return range(CUTS[b + 1] - CUTS[b])
 
-    def unload(q, w):
-        r, b0, b1 = map(int, w)
-        k, e = packed[w]
-        wait(q, e)
-        ready[r, b0] = copy(q, T.c0s[:, r * 256 + b0 * 64:r * 256 + b1 * 64], PB[k][:, 0:(b1 - b0) * 64])
-        freed[k].append(ready[r, b0])
+    def units(b):
+        return range(sum(x + "1%d" % b in steps for x in "ABCDEF") or len(blocks(b)))
 
-    def expand(b):
-        if WIDE[0]:
-            ap, e = picks(0, b)
-            wait("s", e_hf, e)
-            e_v0[b] = [copy("s", PA[b][:, left], ap)]
-            return
-        if rank == 0:
-            wait("t", gathered[0, b])
-            e_v0[b] = [ev(ten.matmul(PA[b][:, left], T.ex[:, 0:128], T.gat[:, col[b]], True, True))]
-            return
-        b0, b1 = v0_piece[b]
-        n = (b1 - b0) * C // 4
-        wait("t", came[0, b])
-        cuts = sorted(set(x for x in range(b * C, (b + 1) * C + 1) if x % C == 0 or (x - b0 * C) % n == 0))
-        e_v0[b] = []
-        for x0, x1 in zip(cuts, cuts[1:]):
-            a, o = divmod(x0 - b0 * C, n)
-            e_v0[b].append(ev(ten.matmul(PA[b][:, x0 - b * C:x1 - b * C], T.ex[:, 128 * a:128 * a + 128],
-                                         T.c0l[:, b0 * 64 + o:b0 * 64 + o + x1 - x0], True, True)))
+    def place(b, j, k):
+        m, n = len(blocks(b)), U * len(blocks(b)) // len(units(b))
+        if j < m:
+            return CUTS[b] + j, slice(k * U, k * U + n)
+        return CUTS[LENDER[b]] + j - m, slice(3 * U + k % 2 * n, 3 * U + (k % 2 + 1) * n)
 
-    def picks(s, b, j=None):
-        m = s * K + b * C
-        m = slice(m, m + C) if j is None else slice(m + j, m + C, 2)
+    last = {}
+
+    def touch(q, u, who, ins):
+        if u in last and last[u][0] != who:
+            wait(q, last[u][1])
+        last[u] = (who, ev(ins()))
+        return last[u][1]
+
+    def picks(s, b, j):
+        m = slice(s * K + CUTS[b] * U + j, s * K + CUTS[b + 1] * U, len(units(b)))
         if s == rank:
             return T.gat[:, m], gathered[rank, b]
         return T.land[:, m], came[s, b]
 
-    def bank(b):
-        assert WIDE[0] or len(freed[b]) == len([k for k in range(len(plan(0))) if rank == 0 and k % NC == b])
-        return freed[b]
-
-    def v0_event(b):
-        if b in e_v0 or not WIDE[0]:
-            return e_v0[b]
-        assert "e%d" % b not in steps
-        return None
-
-    def m1(b):
-        ap, e = picks(1, b)
-        v0, es = PA[b][:, left], v0_event(b)
-        if es is None:
-            v0, e0 = picks(0, b)
-            es = [e0]
-        wait("v", *es, e)
-        if str(b) in WHOLE[rank]:
-            e = ev(vec.tensor_tensor(T.p1[:, col[b]], v0, ap, A.mult))
-            wait("t", e, *bank(b))
-            e_mm[1, b] = ev(ten.matmul(PB[b][:, left], T.sf[:], T.p1[:, col[b]], True, True))
-        else:
-            e = ev(vec.tensor_tensor(PA[b][:, right], v0, ap, A.mult))
-            wait("s", e)
-            e_hi[b] = ev(act.activation(T.hi[:, col[b]], PA[b][:, right], ActivationFunctionType.Copy))
-
-    def lo(b):
-        wait("v", e_hi[b])
-        e = ev(vec.tensor_tensor(T.lo[:, col[b]], PA[b][:, right], T.hi[:, col[b]], A.subtract))
-        wait("t", e_hi[b], *bank(b))
-        ten.matmul(PB[b][:, left], T.sb[:], T.hi[:, col[b]], True, False)
-        wait("t", e)
-        e_mm[1, b] = ev(ten.matmul(PB[b][:, left], T.sb[:], T.lo[:, col[b]], False, True))
-
-    def m2(b):
-        ap, e = picks(2, b)
-        wait("v", e_mm[1, b], e)
-        e = ev(vec.tensor_tensor(T.p2[:, col[b]], PB[b][:, left], ap, A.mult))
-        wait("t", e)
-        e_mm[2, b] = ev(ten.matmul(PB[b][:, right], T.sf[:], T.p2[:, col[b]], True, True))
-
-    def m3(b):
-        ap, e = picks(3, b)
-        wait("v", e_mm[2, b], e)
-        e = ev(vec.tensor_tensor(T.p3[:, col[b]], PB[b][:, right], ap, A.mult))
-        wait("t", e)
-        e = [ev(ten.matmul(PA[b][:, 32 * j:32 * j + 32], T.p3[:, b * C + j:(b + 1) * C:2], so, True, True))
-             for j in range(2)]
-        for j in range(2):
-            e_fin[b, j] = (PA[b][:, 32 * j:32 * j + 32], e)
-
-    halves = {}
-
-    def half(j, w):
+    def stage(q, w):
         s, b = map(int, w)
-        if (b, j) in halves:
-            done, to, e = halves[b, j]
-            assert done == s - 1
-            src, es = to[:, 0:C // 2], [e]
-        else:
-            assert j == 0 or (b, 0) in halves
-            was, o = ((PA[b], 0), (PB[b], 0), (PB[b], C))[s - 1]
-            src, es = was[:, o + j:o + C:2], v0_event(b) if s == 1 else [e_mm[s - 1, b]]
-            to = was if j else PB[b] if s == 1 else PA[b]
-            if es is None:
-                src, e = picks(0, b, j)
-                es = [e]
-        ap, e = picks(s, b, j)
-        wait("v", *es, e)
-        p = (T.p1, T.p2, T.p3)[s - 1][:, b * C + j * C // 2:b * C + (j + 1) * C // 2]
-        e = ev(vec.tensor_tensor(p, src, ap, A.mult))
-        wait("t", e, *bank(b))
+        for j in units(b):
+            ap, e = picks(s, b, j)
+            u, c = place(b, j, 0)
+            dst = PU[u][:, c]
+            wait(q, e_hf, e)
+            e = touch(q, u, (b, j), lambda: act.activation(dst, ap, COPY) if q == "s"
+                      else ten.matmul(dst, T.eye[:], ap, True, True))
+            state[b, j] = (dst, e, 1 - s)
+
+    def unit(j, w):
+        s, b = map(int, w)
+        staged = (b, j) in state
+        src, e0, mode = state[b, j] if staged else picks(0, b, j) + (1,)
+        assert mode == s or (s == 1 and mode == 0)
+        ap, e = picks(mode, b, j)
+        wait("v", e0, e)
+        m, h = len(blocks(b)), len(units(b)) // len(blocks(b))
+        u, c = place(b, j, s)
+        o = (CUTS[b] + j % m) * U
+        buf = (T.p1, T.p2, T.p3)[s - 1]
+        p = buf[:, o + j // m:o + U:h]
+        e = touch("v", u, (b, j), lambda: vec.tensor_tensor(p, src, ap, A.mult)) if staged else ev(
+            vec.tensor_tensor(p, src, ap, A.mult))
         if s < 3:
-            halves[b, j] = (s, to, ev(ten.matmul(to[:, 0:C // 2], T.sf[:], p, True, True)))
-        else:
-            halves[b, j] = (s, to, None)
-            e_fin[b, j] = (to[:, 0:32], [ev(ten.matmul(to[:, 0:32], p, so, True, True))])
+            wait("t", e)
+            dst = PU[u][:, c]
+            state[b, j] = (dst, touch("t", u, (b, j), lambda: ten.matmul(dst, T.sf[:], p, True, True)), s + 1)
+            return
+        state[b, j] = (None, e, 4)
+        both = [state[b, k] for k in units(b) if k % m == j % m]
+        if all(x[2] == 4 for x in both):
+            wait("t", *[x[1] for x in both])
+            u = CUTS[b] + j % m
+            dst = PU[u][:, 0:32]
+            state[b, j % m] = (dst, touch("t", u, (b, j % m),
+                                          lambda: ten.matmul(dst, buf[:, o:o + U], so, True, True)), None)
 
     def out(b):
         queues = "y" if busy[0] else "ys"
-        for j in range(2):
-            ap, es = e_fin[b, j]
-            wait("v", *es)
-            e = ev(vec.transpose(T.yb[:, 64 * b + j:64 * b + 64:2], ap))
+        m, o = len(blocks(b)), CUTS[b] * 32
+        for j in blocks(b):
+            ap, e, mode = state[b, j]
+            assert mode is None
+            wait("v", e)
+            e = touch("v", CUTS[b] + j, (b, j), lambda: vec.transpose(T.yb[:, o + j:o + 32 * m:m], ap))
             for q in queues:
                 wait(q, e)
         for a in range(4):
-            o = b * C + 64 * a
+            y0 = CUTS[b] * U + 32 * m * a
             names[queues[a % len(queues)]].dma_start(
-                T.y[:, o:o + 64], T.yb[32 * a:32 * a + 32, 64 * b:64 * b + 64]).then_inc(T.sem["st"], 16)
+                T.y[:, y0:y0 + 32 * m], T.yb[32 * a:32 * a + 32, o:o + 32 * m]).then_inc(T.sem["st"], 16)
             stored.append(16)
 
-    two = {"m1": m1, "lo": lo, "m2": m2, "m3": m3, "ou": out}
-    one = {"h": hash_all, "x": hash1, "y": hash2, "z": hash3, "p": pack, "e": lambda w: expand(int(w)),
-           "v": lambda w: gather("v", w), "s": lambda w: gather("s", w),
-           "U": lambda w: unload("v", w), "u": lambda w: unload("s", w),
-           "A": lambda w: half(0, w), "B": lambda w: half(1, w)}
-    steps = PROG[rank].split()
+    def whole(w):
+        for j in units(int(w[1])):
+            unit(j, w)
+
+    one = {"h": hash_all, "x": hash1, "y": hash2, "z": hash3, "m": whole, "o": lambda w: out(int(w)),
+           "e": lambda w: stage("s", w), "t": lambda w: stage("t", w),
+           "v": lambda w: gather("v", w), "s": lambda w: gather("s", w)}
     busy = [True]
     for i, step in enumerate(steps):
-        busy[0] = any(w[0] in "sule" for w in steps[i:])
-        if step[:2] in two:
-            two[step[:2]](int(step[2]))
+        busy[0] = any(w[0] in "se" for w in steps[i:])
+        if step[0] in "ABCDEF":
+            unit("ABCDEF".index(step[0]), step[1:])
         else:
             one[step[0]](step[1:])
 
+    call = []
     for i, (r, c0, c1, way) in enumerate(plan(rank)):
-        dst = T.cores[r]
-        if rank == 0 and not WIDE[0]:
-            wait("g", ready[r, c0])
-            send(dst, T.c0l[:, c0 * 64:c1 * 64], T.c0s[:, r * 256 + c0 * 64:r * 256 + c1 * 64], "ma0_%d" % c0,
-                 topo.engines(core, dst))
-            continue
         wait("g", *sorted(set(gathered[r, b] for b in range(c0, c1))))
-        src = T.gat[:, r * K + c0 * C:r * K + c1 * C]
+        src = cols(T.gat, r, c0, c1)
         if way == "d":
-            send(dst, T.land[:, rank * K + c0 * C:rank * K + c1 * C], src, "ma%d_%d" % (rank, c0), topo.engines(core, dst))
+            call.append(transfer([T.cores[r]], [cols(T.land, rank, c0, c1)], src, "ma%d_%d" % (rank, c0),
+                                 topo.engines(core, T.cores[r])))
         else:
-            send(relay(rank, r, way, T, topo), held(T, rank, r, c0, c1, way), src, "e%d" % (16 * rank + i),
-                 first_engines(rank, r, way, T, topo))
+            call.append(transfer([relay(rank, way, T, topo)], [src], src, "e%d" % i, first_engines(rank, r, way, T, topo)))
+        if PLAN[rank].split()[i][-1] != "+":
+            assert len(call) == 1 or (plan(rank)[i - 1][3] == "d") != (way == "d")
+            assert len(call) < 3
+            g.remote_dma_fused(call, local_sem=T.sem["ls"])
+            call = []
     wait("y", ("st", sum(stored)))
     wait("g", ("ls", sent[0]))

from concourse.bass import DstId, RemoteDMATransfer
from concourse.mybir import AluOpType, ActivationFunctionType

N = 4
K = 1024
U = 128
L = K // 16
A = AluOpType
COPY = ActivationFunctionType.Copy

SCRATCH = {
    "idw": ("sbuf", [128, N * L], "int32"),
    "hi": ("sbuf", [128, K], "bfloat16"),
    "lo": ("sbuf", [128, K], "bfloat16"),
    "sb": ("sbuf", [128, 128], "bfloat16"),
    "idl": ("sbuf", [128, N * L], "uint16"),
    "hri": ("sbuf", [128, 256], "int32"),
    "hrf": ("sbuf", [128, 256], "float32"),
    "one": ("sbuf", [128, 1], "float32"),
    "hsf": ("sbuf", [128, 2], "float32"),
    "win": ("sbuf", [128, 4096], "bfloat16"),
    "t1": ("sbuf", [128, N * L], "int32"),
    "t2": ("sbuf", [128, N * L], "int32"),
    "offs": ("sbuf", [128, N * L], "uint16"),
    "gat": ("sbuf", [128, N * K], "bfloat16"),
    "land": ("sbuf", [128, N * K], "bfloat16"),
    "p1": ("sbuf", [128, K], "float32"),
    "p2": ("sbuf", [128, K], "float32"),
    "p3": ("sbuf", [128, K], "float32"),
    "yb": ("sbuf", [128, K // 4], "float32"),
    "km": ("sbuf", [128, 128], "float32"),
    "kd": ("sbuf", [128, 128], "float32"),
    "pidx": ("sbuf", [128, 1], "int32"),
    "i1": ("sbuf", [128, 1], "int32"),
    "i2": ("sbuf", [128, 1], "int32"),
    "keyp": ("sbuf", [128, 1], "float32"),
    "sf": ("sbuf", [128, 128], "float32"),
    "eye": ("sbuf", [128, 128], "bfloat16"),
}
for _b in range(K // U):
    SCRATCH["pu%d" % _b] = ("psum", [128, 512], "float32")
SEMAPHORES = (["e%d" % i for i in range(125)] + ["ida%d" % r for r in range(N)]
              + ["ma%d_%d" % (q, b) for q in range(N) for b in range(4)] + ["ls", "st", "wi", "idr", "idb"])

CUTS = [0, 2, 4, 6, 8]
LATE = [16]
LATE_BY = ["abc"]
LENDER = [3, 3, 0, 0, 0]
NARROW = [0]
ID_CALLS = ["01 l 2"]
IDS_TO = {0: '231', 1: '320', 2: '013', 3: '102'}
PLAN = {0: '201d 301d 101d 223a 323a 123a 112d 312d 212d 234a 334d 134d',
        1: '301d 201d 001d 323a 223a 023a 012d 212d 312d 334a 234d 034d',
        2: '001d 101d 301d 023a 123a 323a 312d 112d 012d 034a 134d 334d',
        3: '101d 001d 201d 123a 023a 223a 212d 012d 112d 134a 034d 234d'}
PROG = {0: 'h0 v002 s024 t00 t01 t02 t03 x2 x3 y2 y3 z2 z3 s201 h1 v301 s101 v223 s323 v123 s112 v312 s212 hl s234 s334 s134 A10 B10 A20 B20 A11 A30 B11 B30 A21 B21 o0 A12 A31 B12 B31 A22 B22 o1 A13 A32 B13 B32 A23 B23 o2 A33 B33 o3',
        1: 'h1 v102 s124 t10 t11 t12 t13 x3 x2 y3 y2 z3 z2 s301 h0 v201 s001 v323 s223 v023 s012 v212 s312 hl s334 s234 s034 A10 B10 A20 B20 A11 A30 B11 B30 A21 B21 o0 A12 A31 B12 B31 A22 B22 o1 A13 A32 B13 B32 A23 B23 o2 A33 B33 o3',
        2: 'h2 v202 s224 x0 x1 y0 y1 z0 z1 s001 h3 v101 s301 v023 s123 v323 s312 v112 s012 hl s034 s134 s334 A10 B10 A20 B20 e01 A11 A30 B11 B30 A21 B21 e02 o0 A12 A31 B12 B31 A22 B22 e03 o1 A13 A32 B13 B32 A23 B23 o2 A33 B33 o3',
        3: 'h3 v302 s324 x1 x0 y1 y0 z1 z0 s101 h2 v001 s201 v123 s023 v223 s212 v012 s112 hl s134 s034 s234 A10 B10 A20 B20 e01 A11 A30 B11 B30 A21 B21 e02 o0 A12 A31 B12 B31 A22 B22 e03 o1 A13 A32 B13 B32 A23 B23 o2 A33 B33 o3'}
OTHER, OWN = "abe", "cfg"


def plan(q):
    return [(int(w[0]), int(w[1]), int(w[2]), w[3]) for w in PLAN[q].split()]


def rounds(q, spec):
    return " ".join("%s%d%d%s" % (r, b, b + 1, way) for b, ways, turned in spec
                    for r, way in zip(IDS_TO[q][::-1] if turned else IDS_TO[q], ways))


def rule(q, on_vector, lag, stager="e", paired=""):
    nc = len(CUTS) - 1
    h = (nc + 1) // 2
    p = ["h%d" % q, "v%d0%d" % (q, h), "s%d%d%d" % (q, h, nc)]
    if q < 2:
        p += ["t%d%d" % (q, b) for b in range(nc)]
    p += [x + r for x in "xyz" for r in IDS_TO[q][:2]]
    for k, (r, c0, c1, way) in enumerate(plan(q)):
        if k == 1:
            p.append("h" + IDS_TO[q][2])
        if LATE[0] and "hl" not in p and CUTS[c0] * U // 16 >= L - LATE[0]:
            p.append("hl")
        p.append("%s%d%d%d" % ("v" if k in on_vector else "s", r, c0, c1))
    w = []
    for b in range(nc):
        if q >= 2 and b:
            w.append((lag * b + .3, stager + "0%d" % b))
        for s in (1, 2, 3):
            t = lag * b + s - (s == 1 and str(b) in paired) * .6
            w += [(t + j * .01, "ABCD"[j] + "%d%d" % (s, b)) for j in range(CUTS[b + 1] - CUTS[b])]
        if str(b) in paired:
            w += [(lag * b + 1.2 + j * .01, "abcd"[j] + "1%d" % b) for j in range(CUTS[b + 1] - CUTS[b])]
        w.append((lag * b + 4.5, "o%d" % b))
    return " ".join(p + [x for _, x in sorted(w)])


def named(q, text):
    return text.translate(str.maketrans("wpqr", str(q) + IDS_TO[q]))


PLANS = ['p01d q01d p12b+ r01d q12d r12d+ p23b q23a+ r23d q34a+ p34d r34d', 'q01d p01d r01d q12d p12b r12d p23a q23a+ r23d r34d q34b p34d']
PROGS = ['xw yw zw vw02 tw0 tw1 sw24 xp tw2 tw3 xq yp yq xr zp zq yr zr vq01 vp12 sp01 sr01 vq23 sp23 vr12 xl sq12 yl zl sr23 sq34 vp34 sr34 A10 B10 A20 B20 B11 A11 A30 B30 A12 B21 B12 A21 B31 A22 A13 B13 B22 A23 B23 A31 B32 o0 A32 A33 B33 o1 o2 o3', 'hw xp sw24 xq yp xr yq sw02 zp yr sp01 zq vq01 zr vp12 vr01 vq23 vr12 sr23 sq12 xl yl zl sp23 sr34 vq34 sp34 t00 A10 B10 A20 B20 A11 B11 A30 B30 A21 B21 A12 B12 B31 A31 A22 A13 B13 B22 A23 B23 o1 B32 A32 A33 B33 o0 o2 o3']


def spell():
    for q in range(N):
        PLAN[q], PROG[q] = named(q, PLANS[q // 2]), named(q, PROGS[q // 2])


spell()


def id_col(q, r, c):
    if r == q:
        return c
    s = "".join(w[1:] for w in PROG[q].split() if w[0] in "hx" and w[1:] not in ("l", str(q))).index(str(r))
    early = L - LATE[0]
    return L + s * early + c if c < early else L + (N - 1) * early + s * LATE[0] + c - early


def relay(q, way, T, topo):
    src = T.cores[q]
    if way == "d":
        return src
    c = [x for x in topo.cores_of(src) if x != src and (topo.die(x) == topo.die(src)) == (way in OWN)]
    c.sort(key=lambda x: not all(topo.may_write(x, d) for d in T.cores))
    return c[(OWN if way in OWN else OTHER).index(way)]


def first_engines(q, r, way, T, topo):
    src = T.cores[q]
    return [e for e in topo.engines(src, relay(q, way, T, topo)) if e not in topo.engines(src, T.cores[r])]


def ids_engines(q, r, T, topo):
    eng = topo.engines(T.cores[q], T.cores[r])
    return [eng[0::2], eng[1::2], eng][IDS_TO[q].index(str(r))]


def cols(buf, s, c0, c1):
    return buf[:, s * K + CUTS[c0] * U:s * K + CUTS[c1] * U]


def relay_program(g, core, T, topo):
    sent = [0]

    def send(r, out_ap, in_ap, sem):
        rid, pid, _se = topo.addr(T.cores[r])
        g.remote_dma(out_ap, in_ap, T.sem[sem], T.sem["ls"], pid, rid, topo.mask(core, T.cores[r]))
        sent[0] += len(topo.engines(core, T.cores[r]))

    for q in range(N):
        for r, way in zip(map(int, IDS_TO[q]), LATE_BY[0]):
            if LATE[0] and relay(q, way, T, topo) == core:
                g.wait_ge(T.sem["idr"], len(first_engines(q, r, way, T, topo)))
                o = id_col(r, q, L - LATE[0])
                idl = T.idl if NARROW[0] else T.idw
                send(r, idl[:, o:o + LATE[0]], idl[:, L - LATE[0]:L], "idb")
        for i, (r, c0, c1, way) in enumerate(plan(q)):
            if relay(q, way, T, topo) == core:
                g.wait_ge(T.sem["e%d" % i], len(first_engines(q, r, way, T, topo)))
                send(r, cols(T.land, q, c0, c1), cols(T.gat, r, c0, c1), "ma%d_%d" % (q, c0))
    if sent[0]:
        g.wait_ge(T.sem["ls"], sent[0])


def rank_program(g, core, T, topo):
    rank = T.rank_of(core)
    if rank is None:
        relay_program(g, core, T, topo)
        return
    vec, act, ten, sync = g.vector, g.scalar, g.tensor, g.sync
    used = [0]
    seen = set()

    def ev(ins, n=1):
        name = "e%d" % used[0]
        used[0] += 1
        ins.then_inc(T.sem[name], n)
        return (name, n)

    names = {"v": vec, "s": act, "t": ten, "y": sync, "g": g}

    def wait(q, *evs):
        for name, n in evs:
            if (q, name) not in seen:
                seen.add((q, name))
                names[q].wait_ge(T.sem[name], n)

    sent = [0]

    def send(dst, out_ap, in_ap, sem, eng):
        rid, pid, _se = topo.addr(dst)
        g.remote_dma(out_ap, in_ap, T.sem[sem], T.sem["ls"], pid, rid, sum(1 << e for e in eng))
        sent[0] += len(eng)

    steps = PROG[rank].split()
    early = L - LATE[0]
    idl = T.idl if NARROW[0] else T.idw
    e_ld = ev(sync.dma_start(T.idw[:, 0:L], T.ids[:]), 16)
    e_hs = ev(act.dma_start(T.hri[0:1, :], T.hs[:]), 16)
    if rank == 0:
        for p in range(16):
            (act if p % 2 else sync).dma_start(T.win[p:128:16, :], T.mat[p // 4:128:16, :]).then_inc(T.sem["wi"], 16)
        e_mat = ("wi", 256)
    else:
        e_mat = ev(sync.dma_start(T.win[:], T.mat[:]), 16)

    e_p = ev(g.iota(T.pidx[:], [[1, 1]], 0, 1))
    e_km = ev(g.iota(T.km[:], [[1, 32], [0, 4]], 0, 0, allow_small_or_imprecise_dtypes=True))
    if any(w[0] == "t" for w in steps):
        e_kd = ev(g.iota(T.kd[:], [[1, 128]], 0, -1, allow_small_or_imprecise_dtypes=True))
    e_one = ev(vec.memset(T.one[0:1, :], 1.0))
    wait("v", e_p)
    e1 = ev(vec.tensor_scalar(T.i1[:], T.pidx[:], 2, 28, A.logical_shift_right, A.bitwise_and))
    e2 = ev(vec.tensor_scalar(T.i2[:], T.pidx[:], 3, None, A.bitwise_and))
    wait("v", e1, e2)
    e_key = ev(vec.tensor_tensor(T.keyp[:], T.i1[:], T.i2[:], A.add))

    e_ids = e_ld
    if NARROW[0]:
        wait("v", e_ld)
        e_ids = ev(vec.tensor_copy(T.idl[:, 0:L], T.idw[:, 0:L]))
    wait("g", e_ids)
    to = [int(r) for r in IDS_TO[rank]]

    def transfer(cores, outs, src, sem, eng):
        sent[0] += len(eng)
        return RemoteDMATransfer(dst_ids=[DstId(rid=topo.addr(c)[0], pnc=topo.addr(c)[1]) for c in cores],
                                 dma_engine_mask=sum(1 << e for e in eng), remote_sem=T.sem[sem], srcs=[src], dsts=outs)

    tr = {}
    if LATE[0]:
        via = [relay(rank, way, T, topo) for way in sorted(set(LATE_BY[0]))]
        tr["l"] = transfer(via, [idl[:, early:L]] * len(via), idl[:, early:L], "idr",
                           first_engines(rank, to[0], LATE_BY[0][0], T, topo))
    for k, r in enumerate(to):
        o = id_col(r, rank, 0)
        tr[str(k)] = transfer([T.cores[r]], [idl[:, o:o + early]], idl[:, 0:early], "ida%d" % rank,
                              ids_engines(rank, r, T, topo))
    for call in ID_CALLS[0].split():
        if call[0] in tr:
            g.remote_dma_fused([tr[k] for k in call], local_sem=T.sem["ls"])

    PU = [T["pu%d" % u] for u in range(K // U)]
    wait("v", e_hs)
    e_hr = ev(vec.tensor_copy(T.hrf[0:1, :], T.hri[0:1, :]))
    wait("t", e_one, e_hr)
    e_ht = [ev(ten.matmul(PU[0][:, k:k + 1], T.hrf[0:1, k:256:2], T.one[0:1, :], True, True)) for k in range(2)]
    wait("v", e_key, e_km)
    e_sf = ev(vec.tensor_scalar(T.sf[:], T.km[:], T.keyp[:, 0:1], None, A.is_equal))
    wait("v", *e_ht)
    e_hf = ev(vec.tensor_copy(T.hsf[:], PU[0][:, 0:2]))
    if any(w[0] == "t" for w in steps):
        wait("v", e_kd)
        wait("t", ev(vec.tensor_scalar(T.eye[:], T.kd[:], 0.0, None, A.is_equal)))
    wait("v", e_hf)
    wait("t", e_hf, e_sf)

    came = {}
    for q in range(N):
        for r, c0, c1, way in plan(q):
            if r == rank:
                for b in range(c0, c1):
                    came[q, b] = ("ma%d_%d" % (q, c0), len(topo.engines(relay(q, way, T, topo), core)))

    so = T.sf[:, 0:128:4]
    hashed, gathered, part, state = {}, {}, {}, {}
    stored = []

    def span(w):
        if w == "l":
            return slice(N * L - (N - 1) * LATE[0], N * L)
        o = id_col(rank, int(w[0]), 0)
        return slice(o, o + (L if int(w[0]) == rank else early * len(w)))

    def hash1(w):
        if w == "l":
            wait("v", ("idb", sum(len(topo.engines(T.cores[r], core)) for r in to)))
        else:
            wait("v", *[e_ids if r == rank else ("ida%d" % r, len(ids_engines(r, rank, T, topo))) for r in map(int, w)])
        part[w] = ev(vec.tensor_scalar(T.t1[:, span(w)], idl[:, span(w)], T.hsf[:, 0:1], T.hsf[:, 1:2], A.mult, A.add))

    def hash2(w):
        wait("v", part.pop(w))
        part["y" + w] = ev(vec.tensor_scalar(T.t2[:, span(w)], T.t1[:, span(w)], 4, 4095,
                                             A.logical_shift_right, A.bitwise_and))

    def hash3(w):
        wait("v", part.pop("y" + w))
        e = ev(vec.tensor_copy(T.offs[:, span(w)], T.t2[:, span(w)]))
        for r in w:
            hashed[r] = e

    def hash_all(w):
        hash1(w)
        hash2(w)
        hash3(w)

    def gather(q, w):
        r, b0, b1 = map(int, w)
        c0, c1 = CUTS[b0] * U // 16, CUTS[b1] * U // 16
        assert r == rank or c0 >= early or c1 <= early
        wait(q, hashed[w[0] if r == rank or c0 < early else "l"], e_mat)
        o = id_col(rank, r, c0)
        src, dst = T.win[:].indirect(T.offs[:, o:o + c1 - c0]), cols(T.gat, r, b0, b1)
        e = ev(vec.tensor_copy(dst, src) if q == "v" else act.activation(dst, src, COPY))
        for b in range(b0, b1):
            gathered[r, b] = e

    def blocks(b):
        return range(CUTS[b + 1] - CUTS[b])

    def units(b):
        return range(sum(x + "1%d" % b in steps for x in "ABCDEF") or len(blocks(b)))

    def place(b, j, k):
        m, n = len(blocks(b)), U * len(blocks(b)) // len(units(b))
        if j < m:
            return CUTS[b] + j, slice(k * U, k * U + n)
        return CUTS[LENDER[b]] + j - m, slice(3 * U + k % 2 * n, 3 * U + (k % 2 + 1) * n)

    last = {}

    def touch(q, u, who, ins):
        if u in last and last[u][0] != who:
            wait(q, last[u][1])
        last[u] = (who, ev(ins()))
        return last[u][1]

    def picks(s, b, j):
        m = slice(s * K + CUTS[b] * U + j, s * K + CUTS[b + 1] * U, len(units(b)))
        if s == rank:
            return T.gat[:, m], gathered[rank, b]
        return T.land[:, m], came[s, b]

    def stage(q, w):
        s, b = map(int, w)
        for j in units(b):
            ap, e = picks(s, b, j)
            u, c = place(b, j, 0)
            dst = PU[u][:, c]
            wait(q, e_hf, e)
            e = touch(q, u, (b, j), lambda: act.activation(dst, ap, COPY) if q == "s"
                      else ten.matmul(dst, T.eye[:], ap, True, True))
            state[b, j] = (dst, e, 1 - s)

    def unit(j, w):
        s, b = map(int, w)
        staged = (b, j) in state
        src, e0, mode = state[b, j] if staged else picks(0, b, j) + (1,)
        assert mode == s or (s == 1 and mode == 0)
        ap, e = picks(mode, b, j)
        wait("v", e0, e)
        m, h = len(blocks(b)), len(units(b)) // len(blocks(b))
        u, c = place(b, j, s)
        o = (CUTS[b] + j % m) * U
        buf = (T.p1, T.p2, T.p3)[s - 1]
        p = buf[:, o + j // m:o + U:h]
        e = touch("v", u, (b, j), lambda: vec.tensor_tensor(p, src, ap, A.mult)) if staged else ev(
            vec.tensor_tensor(p, src, ap, A.mult))
        if s < 3:
            wait("t", e)
            dst = PU[u][:, c]
            state[b, j] = (dst, touch("t", u, (b, j), lambda: ten.matmul(dst, T.sf[:], p, True, True)), s + 1)
            return
        state[b, j] = (None, e, 4)
        both = [state[b, k] for k in units(b) if k % m == j % m]
        if all(x[2] == 4 for x in both):
            wait("t", *[x[1] for x in both])
            u = CUTS[b] + j % m
            dst = PU[u][:, 0:32]
            state[b, j % m] = (dst, touch("t", u, (b, j % m),
                                          lambda: ten.matmul(dst, buf[:, o:o + U], so, True, True)), None)

    def out(b):
        queues = "y" if busy[0] else "ys"
        m, o = len(blocks(b)), CUTS[b] * 32
        for j in blocks(b):
            ap, e, mode = state[b, j]
            assert mode is None
            wait("v", e)
            e = touch("v", CUTS[b] + j, (b, j), lambda: vec.transpose(T.yb[:, o + j:o + 32 * m:m], ap))
            for q in queues:
                wait(q, e)
        for a in range(4):
            y0 = CUTS[b] * U + 32 * m * a
            names[queues[a % len(queues)]].dma_start(
                T.y[:, y0:y0 + 32 * m], T.yb[32 * a:32 * a + 32, o:o + 32 * m]).then_inc(T.sem["st"], 16)
            stored.append(16)

    def whole(w):
        for j in units(int(w[1])):
            unit(j, w)

    one = {"h": hash_all, "x": hash1, "y": hash2, "z": hash3, "m": whole, "o": lambda w: out(int(w)),
           "e": lambda w: stage("s", w), "t": lambda w: stage("t", w),
           "v": lambda w: gather("v", w), "s": lambda w: gather("s", w)}
    busy = [True]
    for i, step in enumerate(steps):
        busy[0] = any(w[0] in "se" for w in steps[i:])
        if step[0] in "ABCDEF":
            unit("ABCDEF".index(step[0]), step[1:])
        else:
            one[step[0]](step[1:])

    call = []
    for i, (r, c0, c1, way) in enumerate(plan(rank)):
        wait("g", *sorted(set(gathered[r, b] for b in range(c0, c1))))
        src = cols(T.gat, r, c0, c1)
        if way == "d":
            call.append(transfer([T.cores[r]], [cols(T.land, rank, c0, c1)], src, "ma%d_%d" % (rank, c0),
                                 topo.engines(core, T.cores[r])))
        else:
            call.append(transfer([relay(rank, way, T, topo)], [src], src, "e%d" % i, first_engines(rank, r, way, T, topo)))
        if PLAN[rank].split()[i][-1] != "+":
            assert len(call) == 1 or (plan(rank)[i - 1][3] == "d") != (way == "d")
            assert len(call) < 3
            g.remote_dma_fused(call, local_sem=T.sem["ls"])
            call = []
    wait("y", ("st", sum(stored)))
    wait("g", ("ls", sent[0]))
